import numpy as np
import ml_dtypes


def mxq(x, axis, fmt="e4m3"):
    dtype, down = {"e4m3": (ml_dtypes.float8_e4m3fn, 7), "e5m2": (ml_dtypes.float8_e5m2, 14)}[fmt]
    v = np.moveaxis(np.asarray(x, np.float32).astype(ml_dtypes.bfloat16).astype(np.float64), axis, -1)
    blocks = v.reshape(v.shape[:-1] + (-1, 32))
    amax = np.abs(blocks).max(-1, keepdims=True)
    byte = np.maximum(np.where(amax > 0, np.frexp(amax)[1] - 1 + 127, 0) - down, 1)
    scale = np.exp2(byte - 127.0)
    codes = (blocks / scale).astype(np.float32).astype(dtype).astype(np.float64)
    return np.moveaxis((codes * scale).reshape(v.shape), -1, axis)


WIDE = False


def mx_kscale(k):
    if not WIDE:
        return np.ones(k)
    levels = np.array([10, -10, 5, -5, 0])
    if k % 512:
        return np.exp2(np.random.permutation(np.resize(levels, k // 32))).repeat(32)
    a = np.empty((k // 512, 16))
    for p in range(k // 512):
        a[p, :8] = np.random.permutation(np.resize(levels, 8))
        for g in range(8):
            far = levels[np.abs(levels - a[p, g]) >= 10]
            a[p, g + 8] = far[np.random.randint(len(far))]
    return np.exp2(a.ravel()).repeat(32)


def f64(x):
    return np.asarray(x).astype(np.float64)


def striped(idx):
    return np.tile(idx.reshape(-1, 16).T, (8, 1)).astype(np.uint16)


def unstriped(offs):
    return offs[:16].T.reshape(-1).astype(np.int64)


E2M1 = np.array([0.0, 0.5, 1.0, 1.5, 2.0, 3.0, 4.0, 6.0, -0.0, -0.5, -1.0, -1.5, -2.0, -3.0, -4.0, -6.0])


def pack_weight(w, fmt):
    k, n = w.shape
    w = f64(np.asarray(w, np.float32).astype(ml_dtypes.bfloat16)).reshape(k // 32, 32, n)
    amax = np.abs(w).max(1)
    if fmt == "e4m3":
        byte = np.frexp(amax)[1] - 1 + 127 - 7
    else:
        mant, ex = np.frexp(amax / 6.0)
        byte = np.where(mant > 0.5, ex, ex - 1) + 127
    byte = np.clip(np.where(amax > 0, byte, 1), 1, 254)
    scaled = (w * np.exp2(127.0 - byte)[:, None, :]).reshape(k, n).astype(np.float32)
    by_word = np.ascontiguousarray(scaled.reshape(k // 512, 128, 4, n).transpose(0, 1, 3, 2))
    if fmt == "e4m3":
        words = by_word.astype(ml_dtypes.float8_e4m3fn).view(np.uint8)
    else:
        c = by_word.astype(ml_dtypes.float4_e2m1fn).view(np.uint8) & 0xF
        words = (c[..., 0::2] | (c[..., 1::2] << 4)).reshape(k // 512, 128, 2 * n)
    return np.ascontiguousarray(words), np.ascontiguousarray(byte.astype(np.uint8).reshape(k // 512, 16, n))


def unpack_weight(words, scales, fmt):
    g, _, n = scales.shape
    words = np.ascontiguousarray(words).reshape(g, 128, n, -1)
    if fmt == "e4m3":
        vals = words.view(ml_dtypes.float8_e4m3fn).astype(np.float64)
    else:
        nib = np.empty((g, 128, n, 4), np.uint8)
        nib[..., 0::2] = words & 0xF
        nib[..., 1::2] = words >> 4
        vals = E2M1[nib]
    vals = vals * np.repeat(np.exp2(scales.astype(np.float64) - 127.0), 8, axis=1)[..., None]
    return vals.transpose(0, 1, 3, 2).reshape(g * 512, n)


def relu2(v):
    return np.maximum(v, 0.0) ** 2


K, T, E, G, H, N = 1024, 512, 6, 2, 512, 512


def setup_inputs():
    n = np.random.standard_normal
    s = mx_kscale(K)
    u = mx_kscale(H)
    chosen = np.random.permutation(E)[:G]
    x = pack_weight(n((K, T)) * s[:, None], "e4m3")
    w1 = pack_weight(n((K, E * H)) / np.sqrt(K) / s[:, None] * np.tile(u, E), "e4m3")
    w2 = pack_weight(n((H, E * N)) / np.sqrt(H) / u[:, None] ** 2, "e4m3")
    return {
        "x_words": x[0],
        "x_scales": x[1],
        "w1_words": w1[0],
        "w1_scales": w1[1],
        "w2_words": w2[0],
        "w2_scales": w2[1],
        "gate": np.stack([np.tile(r, (128, 1)) for r in np.random.uniform(0.2, 1.0, (G, T))]).astype(np.float32),
        "offs": striped((chosen[:, None] * H + np.arange(H)).reshape(-1)),
        "offs2": striped((chosen[:, None] * N + np.arange(N)).reshape(-1)),
    }


def reference(x_words, x_scales, w1_words, w1_scales, w2_words, w2_scales, gate, offs, offs2):
    idx, idx2 = unstriped(offs), unstriped(offs2)
    x = unpack_weight(x_words, x_scales, "e4m3")
    w1 = unpack_weight(w1_words, w1_scales, "e4m3")[:, idx]
    w2 = unpack_weight(w2_words, w2_scales, "e4m3")[:, idx2]
    y = np.zeros((N, T))
    for r in range(G):
        h = f64(gate[r, :1]) * relu2(w1[:, r * H:(r + 1) * H].T @ x)
        y = y + w2[:, r * N:(r + 1) * N].T @ mxq(h, 0, "e4m3")
    return y

@@ -1,0 +1,199 @@
+from contextlib import ExitStack
+
+import concourse.mybir as mybir
+from concourse.masks import make_identity
+
+K, T, E, G, H, N = 1024, 512, 6, 2, 512, 512
+FLOPS = 2 * G * T * (K * H + H * N)
+
+F32 = mybir.dt.float32
+BF16 = mybir.dt.bfloat16
+I32 = mybir.dt.int32
+U32 = mybir.dt.uint32
+U16 = mybir.dt.uint16
+U8 = mybir.dt.uint8
+FP8X4 = mybir.dt.float8_e4m3fn_x4
+MULT = mybir.AluOpType.mult
+RELU = mybir.ActivationFunctionType.Relu
+
+P = 128
+PASSES = K // 512
+TILES = T // P
+COLS = E * H
+X_ROW = 8
+W2_ROW = 12
+GATE_STEP = 5
+GATE_COL = (0, 104)
+
+
+def tile_moe_wsel_b_relu2_p_kernel(
+    tc, x_words, x_scales, w1_words, w1_scales, w2_words, w2_scales, gate, offs, offs2, out
+):
+    nc = tc.nc
+    with ExitStack() as ctx:
+        keep = ctx.enter_context(tc.tile_pool(name="keep", bufs=1))
+        ring = ctx.enter_context(tc.tile_pool(name="ring", bufs=4))
+        psum = ctx.enter_context(tc.psum_pool(name="psum", bufs=8))
+
+        def words(dram):
+            return dram.rearrange("p n d -> p (n d)").bitcast(I32)
+
+        def bank():
+            return psum.tile([P, 512], F32, name="bank")
+
+        list1 = keep.tile([P, G * H // 16], U16, name="list1")
+        list2 = keep.tile([P, G * N // 16], U16, name="list2")
+        w1_all = [keep.tile([P, COLS], I32, name=f"w1_all{s}", align_bytes=64) for s in range(PASSES)]
+        w2_all = keep.tile([P, COLS], I32, name="w2_all", align_bytes=64)
+        x_w = [keep.tile([P, T], I32, name=f"x_w{s}", align_bytes=64) for s in range(PASSES)]
+        w1s_all = keep.tile([P, COLS], U8, name="w1s_all", align_bytes=64)
+        w2s_all = keep.tile([P, COLS], U8, name="w2s_all", align_bytes=64)
+        x_s = keep.tile([P, PASSES * T], U8, name="x_s", align_bytes=64)
+        gate_rows = keep.tile([P, P], F32, name="gate_rows")
+        gate_cols = keep.tile([P, P], F32, name="gate_cols")
+        ident = keep.tile([P, P], F32, name="ident")
+
+        nc.vector.memset(w1s_all[:].bitcast(I32), 0)
+        nc.vector.memset(x_s[:].bitcast(I32), 0)
+        nc.vector.memset(w2s_all[:].bitcast(I32), 0)
+
+        nc.sync.dma_start(list1[:], offs)
+        nc.sync.dma_start(list2[:], offs2)
+        nc.sync.dma_start(w1_all[0][:], words(w1_words[0]))
+        nc.sync.dma_start(w1_all[1][:], words(w1_words[1]))
+        nc.sync.dma_start(x_w[1][:], words(x_words[1]))
+        nc.sync.dma_start(w2_all[:], words(w2_words[0]))
+
+        nc.scalar.dma_start(x_w[0][:], words(x_words[0]))
+        nc.scalar.dma_start(
+            gate_rows[:], gate.rearrange("r p (a c) -> (r p a) c", c=P)[0 : GATE_STEP * P : GATE_STEP, :]
+        )
+        for q in range(4):
+            nc.scalar.dma_start(
+                x_s[32 * q + X_ROW : 32 * q + X_ROW + 4, :].bitcast(I32).rearrange("j (s t) -> j s t", s=PASSES),
+                x_scales[:, 4 * q : 4 * q + 4, :].rearrange("s j t -> j s t").bitcast(I32),
+            )
+        for q in range(4):
+            nc.gpsimd.dma_start(
+                w1s_all[32 * q : 32 * q + 4 * PASSES, :].bitcast(I32),
+                w1_scales[:, 4 * q : 4 * q + 4, :].bitcast(I32),
+            )
+        make_identity(nc, ident[:])
+        for q in range(4):
+            nc.gpsimd.dma_start(
+                w2s_all[32 * q + W2_ROW : 32 * q + W2_ROW + 4, :].bitcast(I32),
+                w2_scales[0, 4 * q : 4 * q + 4, :].bitcast(I32),
+            )
+
+        gate_t = bank()
+        nc.tensor.transpose(gate_t[:, 0:P], gate_rows[:], ident[:])
+        nc.scalar.copy(gate_cols[:], gate_t[:, 0:P])
+
+        w1_w = [keep.tile([P, G * H], U32, name=f"w1_w{s}", align_bytes=64) for s in range(PASSES)]
+        w1_s = keep.tile([P, G * H], U8, name="w1_s", align_bytes=64)
+        w2_w = keep.tile([P, G * N], U32, name="w2_w", align_bytes=64)
+        w2_s = keep.tile([P, G * N], U8, name="w2_s", align_bytes=64)
+
+        def gather_words(dst, src, lst, r):
+            nc.vector.tensor_copy(
+                dst[:, r * 512 : (r + 1) * 512], src[:].bitcast(U32).indirect(lst[:, r * 32 : (r + 1) * 32])
+            )
+
+        nc.vector.tensor_copy(w1_s[:], w1s_all[:].indirect(list1[:]))
+        for r in range(G):
+            gather_words(w1_w[0], w1_all[0], list1, r)
+        nc.vector.tensor_copy(w2_s[:], w2s_all[:].indirect(list2[:]))
+
+        def first_product(acc, tt, r, s):
+            nc.tensor.matmul_mx(
+                out=acc[:],
+                lhsT=x_w[s][:, tt * P : (tt + 1) * P].bitcast(FP8X4),
+                lhsT_scale=x_s[X_ROW:P, s * T + tt * P : s * T + (tt + 1) * P],
+                rhs=w1_w[s][:, r * H : (r + 1) * H].bitcast(FP8X4),
+                rhs_scale=w1_s[4 * s : P, r * H : (r + 1) * H],
+                start=(s == 0),
+                stop=(s == PASSES - 1),
+            )
+
+        units = [(tt, r) for tt in range(TILES) for r in range(G)]
+        pre = {u: bank() for u in units}
+        for tt, r in units:
+            first_product(pre[tt, r], tt, r, 0)
+        for r in range(G):
+            gather_words(w1_w[1], w1_all[1], list1, r)
+        for tt, r in units:
+            first_product(pre[tt, r], tt, r, 1)
+
+        hidden = {}
+
+        def activate(tt, r):
+            pos = ring.tile([P, H], F32, name="pos")
+            nc.scalar.activation(
+                pos[:].rearrange("t (u q e) -> t u q e", u=2, e=2),
+                pre[tt, r][:].rearrange("t (q u e) -> t u q e", u=2, e=2),
+                RELU,
+            )
+            h = ring.tile([P, H], BF16, name="h", align_bytes=64)
+            col = GATE_COL[r] + tt
+            nc.vector.scalar_tensor_tensor(h[:], pos[:], gate_cols[:, col : col + 1], pos[:], MULT, MULT)
+            hidden[tt, r] = h
+
+        codes = {}
+
+        def turn(tt):
+            turned = bank()
+            for r in range(G):
+                for u in range(2):
+                    nc.tensor.transpose(
+                        turned[:, (2 * r + u) * P : (2 * r + u + 1) * P],
+                        hidden[tt, r][:].bitcast(F32)[:, u * P : (u + 1) * P],
+                        ident[:],
+                    )
+            h_t = ring.tile([P, G * P * 4], BF16, name="h_t", align_bytes=64)
+            nc.scalar.copy(
+                h_t[:].bitcast(F32).rearrange("q (r t u) -> q r t u", r=G, u=2),
+                turned[:].rearrange("q (r u t) -> q r t u", r=G, u=2),
+            )
+            h_w = ring.tile([P, G * P], U32, name="h_w", align_bytes=64)
+            h_s = ring.tile([P, G * P], U8, name="h_s", align_bytes=64)
+            nc.vector.quantize_mx(out=h_w[:].bitcast(FP8X4), scales=h_s[:], in_=h_t[:])
+            codes[tt] = (h_w, h_s)
+
+        out_view = out.rearrange("(j p) t -> p j t", p=P)
+
+        def second_product(tt):
+            h_w, h_s = codes[tt]
+            acc = bank()
+            for j in range(N // P):
+                for r in range(G):
+                    cols = slice(r * N + j * P, r * N + (j + 1) * P)
+                    nc.tensor.matmul_mx(
+                        out=acc[:, j * P : (j + 1) * P],
+                        lhsT=w2_w[:, cols].bitcast(FP8X4),
+                        lhsT_scale=w2_s[W2_ROW:P, cols],
+                        rhs=h_w[:, r * P : (r + 1) * P].bitcast(FP8X4),
+                        rhs_scale=h_s[:, r * P : (r + 1) * P],
+                        start=(r == 0),
+                        stop=(r == G - 1),
+                    )
+            res = ring.tile([P, N], F32, name="res")
+            if tt == TILES - 1:
+                nc.vector.tensor_copy(res[:], acc[:])
+            else:
+                nc.scalar.copy(res[:], acc[:])
+            nc.sync.dma_start(
+                out_view[:, :, tt * P : (tt + 1) * P], res[:].rearrange("p (j t) -> p j t", t=P)
+            )
+
+        for tt in range(TILES):
+            for r in range(G):
+                activate(tt, r)
+            if tt >= 1:
+                turn(tt - 1)
+            if tt == 2:
+                for r in range(G):
+                    gather_words(w2_w, w2_all, list2, r)
+        second_product(0)
+        turn(TILES - 1)
+        for tt in range(1, TILES):
+            second_product(tt)

@@ -33,23 +33,24 @@ def tile_moe_wsel_b_relu2_p_kernel(
     with ExitStack() as ctx:
         keep = ctx.enter_context(tc.tile_pool(name="keep", bufs=1))
         ring = ctx.enter_context(tc.tile_pool(name="ring", bufs=4))
-        psum = ctx.enter_context(tc.psum_pool(name="psum", bufs=8))
+        psum = ctx.enter_context(tc.psum_pool(name="psum", bufs=1))
 
         def words(dram):
             return dram.rearrange("p n d -> p (n d)").bitcast(I32)
 
-        def bank():
-            return psum.tile([P, 512], F32, name="bank")
+        def bank(b):
+            return psum.tile([P, 512], F32, name=f"bank{b}", tag=f"bank{b}")
 
         list1 = keep.tile([P, G * H // 16], U16, name="list1")
         list2 = keep.tile([P, G * N // 16], U16, name="list2")
-        w1_all = [keep.tile([P, COLS], I32, name=f"w1_all{s}", align_bytes=64) for s in range(PASSES)]
-        w2_all = keep.tile([P, COLS], I32, name="w2_all", align_bytes=64)
-        x_w = [keep.tile([P, T], I32, name=f"x_w{s}", align_bytes=64) for s in range(PASSES)]
-        w1s_all = keep.tile([P, COLS], U8, name="w1s_all", align_bytes=64)
+        w1_all = [
+            keep.tile([P, COLS], I32, name=f"w1_all{s}", tag=f"w_all{s}", align_bytes=64) for s in range(PASSES)
+        ]
+        x_w = [keep.tile([P, T], I32, name="x_w0", align_bytes=64)]
+        w1s_all = keep.tile([P, COLS], U8, name="w1s_all", tag="w1s_all", align_bytes=64)
         w2s_all = keep.tile([P, COLS], U8, name="w2s_all", align_bytes=64)
         x_s = keep.tile([P, PASSES * T], U8, name="x_s", align_bytes=64)
-        gate_rows = keep.tile([P, P], F32, name="gate_rows")
+        gate_rows = keep.tile([P, P], F32, name="gate_rows", tag="gate_rows", align_bytes=64)
         gate_cols = keep.tile([P, P], F32, name="gate_cols")
         ident = keep.tile([P, P], F32, name="ident")
 
@@ -57,17 +58,21 @@ def tile_moe_wsel_b_relu2_p_kernel(
         nc.vector.memset(x_s[:].bitcast(I32), 0)
         nc.vector.memset(w2s_all[:].bitcast(I32), 0)
 
+        nc.sync.dma_start(x_w[0][:], words(x_words[0]))
+        nc.sync.dma_start(
+            gate_rows[:], gate.rearrange("r p (a c) -> (r p a) c", c=P)[0 : GATE_STEP * P : GATE_STEP, :]
+        )
         nc.sync.dma_start(list1[:], offs)
         nc.sync.dma_start(list2[:], offs2)
         nc.sync.dma_start(w1_all[0][:], words(w1_words[0]))
         nc.sync.dma_start(w1_all[1][:], words(w1_words[1]))
-        nc.sync.dma_start(x_w[1][:], words(x_words[1]))
-        nc.sync.dma_start(w2_all[:], words(w2_words[0]))
 
-        nc.scalar.dma_start(x_w[0][:], words(x_words[0]))
-        nc.scalar.dma_start(
-            gate_rows[:], gate.rearrange("r p (a c) -> (r p a) c", c=P)[0 : GATE_STEP * P : GATE_STEP, :]
-        )
+        make_identity(nc, ident[:])
+        for q in range(4):
+            nc.scalar.dma_start(
+                w1s_all[32 * q : 32 * q + 4 * PASSES, :].bitcast(I32),
+                w1_scales[:, 4 * q : 4 * q + 4, :].bitcast(I32),
+            )
         for q in range(4):
             nc.scalar.dma_start(
                 x_s[32 * q + X_ROW : 32 * q + X_ROW + 4, :].bitcast(I32).rearrange("j (s t) -> j s t", s=PASSES),
@@ -75,59 +80,58 @@ def tile_moe_wsel_b_relu2_p_kernel(
             )
         for q in range(4):
             nc.gpsimd.dma_start(
-                w1s_all[32 * q : 32 * q + 4 * PASSES, :].bitcast(I32),
-                w1_scales[:, 4 * q : 4 * q + 4, :].bitcast(I32),
-            )
-        make_identity(nc, ident[:])
-        for q in range(4):
-            nc.gpsimd.dma_start(
                 w2s_all[32 * q + W2_ROW : 32 * q + W2_ROW + 4, :].bitcast(I32),
                 w2_scales[0, 4 * q : 4 * q + 4, :].bitcast(I32),
             )
 
-        gate_t = bank()
+        gate_t = bank(7)
         nc.tensor.transpose(gate_t[:, 0:P], gate_rows[:], ident[:])
         nc.scalar.copy(gate_cols[:], gate_t[:, 0:P])
 
-        w1_w = [keep.tile([P, G * H], U32, name=f"w1_w{s}", align_bytes=64) for s in range(PASSES)]
-        w1_s = keep.tile([P, G * H], U8, name="w1_s", align_bytes=64)
-        w2_w = keep.tile([P, G * N], U32, name="w2_w", align_bytes=64)
-        w2_s = keep.tile([P, G * N], U8, name="w2_s", align_bytes=64)
+        x_w.append(keep.tile([P, T], I32, name="x_w1", tag="gate_rows", align_bytes=64))
+        nc.sync.dma_start(x_w[1][:], words(x_words[1]))
 
-        def gather_words(dst, src, lst, r):
-            nc.vector.tensor_copy(
-                dst[:, r * 512 : (r + 1) * 512], src[:].bitcast(U32).indirect(lst[:, r * 32 : (r + 1) * 32])
-            )
+        w1_w = {}
+        w2_w = {}
+        w1_s = keep.tile([P, G * H], U8, name="w1_s", align_bytes=64)
+
+        def gather_words(src, lst, r, tag):
+            dst = keep.tile([P, 512], U32, name=f"picked_{tag}", tag=tag, align_bytes=64)
+            nc.vector.tensor_copy(dst[:], src[:].bitcast(U32).indirect(lst[:, r * 32 : (r + 1) * 32]))
+            return dst
 
         nc.vector.tensor_copy(w1_s[:], w1s_all[:].indirect(list1[:]))
         for r in range(G):
-            gather_words(w1_w[0], w1_all[0], list1, r)
-        nc.vector.tensor_copy(w2_s[:], w2s_all[:].indirect(list2[:]))
+            w1_w[0, r] = gather_words(w1_all[0], list1, r, f"w1_w0{r}")
+        w2_all = keep.tile([P, COLS], I32, name="w2_all", tag="w_all0", align_bytes=64)
+        nc.sync.dma_start(w2_all[:], words(w2_words[0]))
 
         def first_product(acc, tt, r, s):
             nc.tensor.matmul_mx(
                 out=acc[:],
                 lhsT=x_w[s][:, tt * P : (tt + 1) * P].bitcast(FP8X4),
                 lhsT_scale=x_s[X_ROW:P, s * T + tt * P : s * T + (tt + 1) * P],
-                rhs=w1_w[s][:, r * H : (r + 1) * H].bitcast(FP8X4),
+                rhs=w1_w[s, r][:].bitcast(FP8X4),
                 rhs_scale=w1_s[4 * s : P, r * H : (r + 1) * H],
                 start=(s == 0),
                 stop=(s == PASSES - 1),
             )
 
         units = [(tt, r) for tt in range(TILES) for r in range(G)]
-        pre = {u: bank() for u in units}
+        pre = {u: bank(b) for b, u in enumerate(units)}
         for tt, r in units:
             first_product(pre[tt, r], tt, r, 0)
-        for r in range(G):
-            gather_words(w1_w[1], w1_all[1], list1, r)
+        w1_w[1, 0] = gather_words(w1_all[1], list1, 0, "w1s_all")
+        w1_w[1, 1] = gather_words(w1_all[1], list1, 1, "w1_w11")
+        w2_s = keep.tile([P, G * N], U8, name="w2_s", tag="w_all1", align_bytes=64)
+        nc.vector.tensor_copy(w2_s[:], w2s_all[:].indirect(list2[:]))
         for tt, r in units:
             first_product(pre[tt, r], tt, r, 1)
 
         hidden = {}
 
         def activate(tt, r):
-            pos = ring.tile([P, H], F32, name="pos")
+            pos = keep.tile([P, H], F32, name=f"pos{tt}{r}", tag=f"pos{tt}{r}", align_bytes=64)
             nc.scalar.activation(
                 pos[:].rearrange("t (u q e) -> t u q e", u=2, e=2),
                 pre[tt, r][:].rearrange("t (q u e) -> t u q e", u=2, e=2),
@@ -140,60 +144,81 @@ def tile_moe_wsel_b_relu2_p_kernel(
 
         codes = {}
 
-        def turn(tt):
-            turned = bank()
-            for r in range(G):
+        def turn(tt, experts, b):
+            n = len(experts)
+            turned = bank(b)
+            for i, r in enumerate(experts):
                 for u in range(2):
                     nc.tensor.transpose(
-                        turned[:, (2 * r + u) * P : (2 * r + u + 1) * P],
+                        turned[:, (2 * i + u) * P : (2 * i + u + 1) * P],
                         hidden[tt, r][:].bitcast(F32)[:, u * P : (u + 1) * P],
                         ident[:],
                     )
-            h_t = ring.tile([P, G * P * 4], BF16, name="h_t", align_bytes=64)
+            h_t = ring.tile([P, n * P * 4], BF16, name="h_t", align_bytes=64)
             nc.scalar.copy(
-                h_t[:].bitcast(F32).rearrange("q (r t u) -> q r t u", r=G, u=2),
-                turned[:].rearrange("q (r u t) -> q r t u", r=G, u=2),
+                h_t[:].bitcast(F32).rearrange("q (r t u) -> q r t u", r=n, u=2),
+                turned[:, 0 : 2 * n * P].rearrange("q (r u t) -> q r t u", r=n, u=2),
             )
-            h_w = ring.tile([P, G * P], U32, name="h_w", align_bytes=64)
-            h_s = ring.tile([P, G * P], U8, name="h_s", align_bytes=64)
+            h_w = keep.tile([P, n * P], U32, name=f"h_w{b}", align_bytes=64)
+            h_s = keep.tile([P, n * P], U8, name=f"h_s{b}", align_bytes=64)
             nc.vector.quantize_mx(out=h_w[:].bitcast(FP8X4), scales=h_s[:], in_=h_t[:])
-            codes[tt] = (h_w, h_s)
+            for i, r in enumerate(experts):
+                codes[tt, r] = (h_w[:, i * P : (i + 1) * P], h_s[:, i * P : (i + 1) * P])
 
         out_view = out.rearrange("(j p) t -> p j t", p=P)
 
+        def second_pass(acc, tt, j, r):
+            h_w, h_s = codes[tt, r]
+            nc.tensor.matmul_mx(
+                out=acc,
+                lhsT=w2_w[r][:, j * P : (j + 1) * P].bitcast(FP8X4),
+                lhsT_scale=w2_s[W2_ROW:P, r * N + j * P : r * N + (j + 1) * P],
+                rhs=h_w.bitcast(FP8X4),
+                rhs_scale=h_s,
+                start=(r == 0),
+                stop=(r == G - 1),
+            )
+
         def second_product(tt):
-            h_w, h_s = codes[tt]
-            acc = bank()
+            acc = bank(2 * tt + 1)
             for j in range(N // P):
                 for r in range(G):
-                    cols = slice(r * N + j * P, r * N + (j + 1) * P)
-                    nc.tensor.matmul_mx(
-                        out=acc[:, j * P : (j + 1) * P],
-                        lhsT=w2_w[:, cols].bitcast(FP8X4),
-                        lhsT_scale=w2_s[W2_ROW:P, cols],
-                        rhs=h_w[:, r * P : (r + 1) * P].bitcast(FP8X4),
-                        rhs_scale=h_s[:, r * P : (r + 1) * P],
-                        start=(r == 0),
-                        stop=(r == G - 1),
-                    )
+                    second_pass(acc[:, j * P : (j + 1) * P], tt, j, r)
             res = ring.tile([P, N], F32, name="res")
-            if tt == TILES - 1:
-                nc.vector.tensor_copy(res[:], acc[:])
-            else:
-                nc.scalar.copy(res[:], acc[:])
+            nc.scalar.copy(res[:], acc[:])
             nc.sync.dma_start(
                 out_view[:, :, tt * P : (tt + 1) * P], res[:].rearrange("p (j t) -> p j t", t=P)
             )
 
-        for tt in range(TILES):
+        last = TILES - 1
+        for tt in range(last):
             for r in range(G):
                 activate(tt, r)
+                if tt == last - 1:
+                    w2_w[r] = gather_words(w2_all, list2, r, f"pos{tt}{r}")
             if tt >= 1:
-                turn(tt - 1)
-            if tt == 2:
-                for r in range(G):
-                    gather_words(w2_w, w2_all, list2, r)
+                turn(tt - 1, range(G), 2 * (tt - 1))
+        activate(last, 0)
         second_product(0)
-        turn(TILES - 1)
-        for tt in range(1, TILES):
-            second_product(tt)
+        activate(last, 1)
+        turn(last - 1, range(G), 2 * (last - 1))
+        second_product(1)
+        turn(last, [0], 2 * last)
+        turn(last, [1], 2 * last + 1)
+        second_product(2)
+        accs = [bank(2 * j) for j in range(N // P)]
+        for r in range(G):
+            for j in range(N // P):
+                second_pass(accs[j][:, 0:P], last, j, r)
+        halves = [keep.tile([P, 2 * P], F32, name=f"half{i}") for i in range(2)]
+        for j in range(N // P):
+            dst = halves[j // 2][:, (j % 2) * P : (j % 2 + 1) * P]
+            if j % 2 == 0:
+                nc.vector.tensor_copy(dst, accs[j][:, 0:P])
+            else:
+                nc.scalar.copy(dst, accs[j][:, 0:P])
+            if j % 2 == 1:
+                nc.sync.dma_start(
+                    out_view[:, j - 1 : j + 1, last * P : (last + 1) * P],
+                    halves[j // 2][:].rearrange("p (j t) -> p j t", t=P),
+                )

@@ -22,6 +22,7 @@ TILES = T // P
 COLS = E * H
 X_ROW = 8
 W2_ROW = 12
+AHEAD = 4
 GATE_STEP = 5
 GATE_COL = (0, 104)
 
@@ -43,68 +44,67 @@ def tile_moe_wsel_b_relu2_p_kernel(
 
         list1 = keep.tile([P, G * H // 16], U16, name="list1")
         list2 = keep.tile([P, G * N // 16], U16, name="list2")
-        w1_all = [
-            keep.tile([P, COLS], I32, name=f"w1_all{s}", tag=f"w_all{s}", align_bytes=64) for s in range(PASSES)
-        ]
-        x_w = [keep.tile([P, T], I32, name="x_w0", align_bytes=64)]
-        w1s_all = keep.tile([P, COLS], U8, name="w1s_all", tag="w1s_all", align_bytes=64)
+        w1_all = [keep.tile([P, COLS], I32, name=f"w1_all{s}", align_bytes=64) for s in range(PASSES)]
+        w2_all = keep.tile([P, COLS], I32, name="w2_all", align_bytes=64)
+        x_w = [keep.tile([P, T], I32, name=f"x_w{s}", align_bytes=64) for s in range(PASSES)]
+        w1s_all = keep.tile([P, COLS], U8, name="w1s_all", align_bytes=64)
         w2s_all = keep.tile([P, COLS], U8, name="w2s_all", align_bytes=64)
         x_s = keep.tile([P, PASSES * T], U8, name="x_s", align_bytes=64)
-        gate_rows = keep.tile([P, P], F32, name="gate_rows", tag="gate_rows", align_bytes=64)
+        gate_rows = keep.tile([P, P], F32, name="gate_rows")
         gate_cols = keep.tile([P, P], F32, name="gate_cols")
         ident = keep.tile([P, P], F32, name="ident")
 
+        nc.vector.memset(w2s_all[:].bitcast(I32), 0)
         nc.vector.memset(w1s_all[:].bitcast(I32), 0)
         nc.vector.memset(x_s[:].bitcast(I32), 0)
-        nc.vector.memset(w2s_all[:].bitcast(I32), 0)
-
-        nc.sync.dma_start(x_w[0][:], words(x_words[0]))
-        nc.sync.dma_start(
-            gate_rows[:], gate.rearrange("r p (a c) -> (r p a) c", c=P)[0 : GATE_STEP * P : GATE_STEP, :]
-        )
-        nc.sync.dma_start(list1[:], offs)
-        nc.sync.dma_start(list2[:], offs2)
-        nc.sync.dma_start(w1_all[0][:], words(w1_words[0]))
-        nc.sync.dma_start(w1_all[1][:], words(w1_words[1]))
-
         make_identity(nc, ident[:])
+
         for q in range(4):
             nc.scalar.dma_start(
-                w1s_all[32 * q : 32 * q + 4 * PASSES, :].bitcast(I32),
-                w1_scales[:, 4 * q : 4 * q + 4, :].bitcast(I32),
-            )
-        for q in range(4):
-            nc.scalar.dma_start(
-                x_s[32 * q + X_ROW : 32 * q + X_ROW + 4, :].bitcast(I32).rearrange("j (s t) -> j s t", s=PASSES),
-                x_scales[:, 4 * q : 4 * q + 4, :].rearrange("s j t -> j s t").bitcast(I32),
-            )
-        for q in range(4):
-            nc.gpsimd.dma_start(
                 w2s_all[32 * q + W2_ROW : 32 * q + W2_ROW + 4, :].bitcast(I32),
                 w2_scales[0, 4 * q : 4 * q + 4, :].bitcast(I32),
             )
+        nc.sync.dma_start(list2[:], offs2)
+        nc.sync.dma_start(list1[:], offs)
+        nc.sync.dma_start(w1_all[0][:], words(w1_words[0]))
+        for q in range(4):
+            nc.sync.dma_start(
+                w1s_all[32 * q : 32 * q + 4 * PASSES, :].bitcast(I32),
+                w1_scales[:, 4 * q : 4 * q + 4, :].bitcast(I32),
+            )
+        nc.sync.dma_start(
+            gate_rows[:], gate.rearrange("r p (a c) -> (r p a) c", c=P)[0 : GATE_STEP * P : GATE_STEP, :]
+        )
+        nc.sync.dma_start(w1_all[1][:], words(w1_words[1]))
+        for q in range(4):
+            nc.sync.dma_start(
+                x_s[32 * q + X_ROW : 32 * q + X_ROW + 4, :].bitcast(I32).rearrange("j (s t) -> j s t", s=PASSES),
+                x_scales[:, 4 * q : 4 * q + 4, :].rearrange("s j t -> j s t").bitcast(I32),
+            )
+        for s in range(PASSES):
+            nc.sync.dma_start(x_w[s][:], words(x_words[s]))
+        nc.sync.dma_start(w2_all[:], words(w2_words[0]))
 
-        gate_t = bank(7)
+        gate_t = bank(4)
         nc.tensor.transpose(gate_t[:, 0:P], gate_rows[:], ident[:])
         nc.scalar.copy(gate_cols[:], gate_t[:, 0:P])
-
-        x_w.append(keep.tile([P, T], I32, name="x_w1", tag="gate_rows", align_bytes=64))
-        nc.sync.dma_start(x_w[1][:], words(x_words[1]))
 
         w1_w = {}
         w2_w = {}
         w1_s = keep.tile([P, G * H], U8, name="w1_s", align_bytes=64)
+        w2_s = keep.tile([P, G * N], U8, name="w2_s", align_bytes=64)
 
         def gather_words(src, lst, r, tag):
             dst = keep.tile([P, 512], U32, name=f"picked_{tag}", tag=tag, align_bytes=64)
             nc.vector.tensor_copy(dst[:], src[:].bitcast(U32).indirect(lst[:, r * 32 : (r + 1) * 32]))
             return dst
 
-        nc.vector.tensor_copy(w1_s[:], w1s_all[:].indirect(list1[:]))
+        nc.vector.tensor_copy(w2_s[:], w2s_all[:].indirect(list2[:]))
         for r in range(G):
             w1_w[0, r] = gather_words(w1_all[0], list1, r, f"w1_w0{r}")
-        w2_all = keep.tile([P, COLS], I32, name="w2_all", tag="w_all0", align_bytes=64)
-        nc.sync.dma_start(w2_all[:], words(w2_words[0]))
+        nc.vector.tensor_copy(w1_s[:], w1s_all[:].indirect(list1[:]))
+        for r in range(G):
+            w1_w[1, r] = gather_words(w1_all[1], list1, r, f"w1_w1{r}")
 
         def first_product(acc, tt, r, s):
             nc.tensor.matmul_mx(
@@ -118,15 +118,10 @@ def tile_moe_wsel_b_relu2_p_kernel(
             )
 
         units = [(tt, r) for tt in range(TILES) for r in range(G)]
-        pre = {u: bank(b) for b, u in enumerate(units)}
-        for tt, r in units:
-            first_product(pre[tt, r], tt, r, 0)
-        w1_w[1, 0] = gather_words(w1_all[1], list1, 0, "w1s_all")
-        w1_w[1, 1] = gather_words(w1_all[1], list1, 1, "w1_w11")
-        w2_s = keep.tile([P, G * N], U8, name="w2_s", tag="w_all1", align_bytes=64)
-        nc.vector.tensor_copy(w2_s[:], w2s_all[:].indirect(list2[:]))
-        for tt, r in units:
-            first_product(pre[tt, r], tt, r, 1)
+        pre = {u: bank(b) for b, u in enumerate(units[:AHEAD])}
+        for tt, r in units[:AHEAD]:
+            for s in range(PASSES):
+                first_product(pre[tt, r], tt, r, s)
 
         hidden = {}
 
@@ -137,6 +132,11 @@ def tile_moe_wsel_b_relu2_p_kernel(
                 pre[tt, r][:].rearrange("t (q u e) -> t u q e", u=2, e=2),
                 RELU,
             )
+            later = units.index((tt, r)) + AHEAD
+            if later < len(units):
+                pre[units[later]] = bank(later % AHEAD)
+                for s in range(PASSES):
+                    first_product(pre[units[later]], *units[later], s)
             h = ring.tile([P, H], BF16, name="h", align_bytes=64)
             col = GATE_COL[r] + tt
             nc.vector.scalar_tensor_tensor(h[:], pos[:], gate_cols[:, col : col + 1], pos[:], MULT, MULT)
@@ -159,8 +159,8 @@ def tile_moe_wsel_b_relu2_p_kernel(
                 h_t[:].bitcast(F32).rearrange("q (r t u) -> q r t u", r=n, u=2),
                 turned[:, 0 : 2 * n * P].rearrange("q (r u t) -> q r t u", r=n, u=2),
             )
-            h_w = keep.tile([P, n * P], U32, name=f"h_w{b}", align_bytes=64)
-            h_s = keep.tile([P, n * P], U8, name=f"h_s{b}", align_bytes=64)
+            h_w = keep.tile([P, n * P], U32, name=f"h_w{tt}{experts[0]}", align_bytes=64)
+            h_s = keep.tile([P, n * P], U8, name=f"h_s{tt}{experts[0]}", align_bytes=64)
             nc.vector.quantize_mx(out=h_w[:].bitcast(FP8X4), scales=h_s[:], in_=h_t[:])
             for i, r in enumerate(experts):
                 codes[tt, r] = (h_w[:, i * P : (i + 1) * P], h_s[:, i * P : (i + 1) * P])
@@ -180,7 +180,7 @@ def tile_moe_wsel_b_relu2_p_kernel(
             )
 
         def second_product(tt):
-            acc = bank(2 * tt + 1)
+            acc = bank(6 + tt % 2)
             for j in range(N // P):
                 for r in range(G):
                     second_pass(acc[:, j * P : (j + 1) * P], tt, j, r)
@@ -191,22 +191,25 @@ def tile_moe_wsel_b_relu2_p_kernel(
             )
 
         last = TILES - 1
-        for tt in range(last):
-            for r in range(G):
-                activate(tt, r)
-                if tt == last - 1:
-                    w2_w[r] = gather_words(w2_all, list2, r, f"pos{tt}{r}")
-            if tt >= 1:
-                turn(tt - 1, range(G), 2 * (tt - 1))
-        activate(last, 0)
+        activate(0, 0)
+        activate(0, 1)
+        activate(1, 0)
+        w2_w[0] = gather_words(w2_all, list2, 0, "pos10")
+        turn(0, range(G), 4)
+        activate(1, 1)
+        w2_w[1] = gather_words(w2_all, list2, 1, "pos11")
+        activate(2, 0)
+        turn(1, range(G), 5)
         second_product(0)
-        activate(last, 1)
-        turn(last - 1, range(G), 2 * (last - 1))
+        activate(2, 1)
+        activate(last, 0)
         second_product(1)
-        turn(last, [0], 2 * last)
-        turn(last, [1], 2 * last + 1)
+        turn(2, range(G), 4)
+        activate(last, 1)
+        turn(last, [0], 5)
         second_product(2)
-        accs = [bank(2 * j) for j in range(N // P)]
+        turn(last, [1], 4)
+        accs = [bank(j) for j in range(N // P)]
         for r in range(G):
             for j in range(N // P):
                 second_pass(accs[j][:, 0:P], last, j, r)

@@ -15,6 +15,8 @@ U8 = mybir.dt.uint8
 FP8X4 = mybir.dt.float8_e4m3fn_x4
 MULT = mybir.AluOpType.mult
 RELU = mybir.ActivationFunctionType.Relu
+SQUARE = mybir.ActivationFunctionType.Square
+COPY = mybir.ActivationFunctionType.Copy
 
 P = 128
 PASSES = K // 512
@@ -23,6 +25,9 @@ COLS = E * H
 X_ROW = 8
 W2_ROW = 12
 AHEAD = 4
+PACE = 2
+EARLY = 4
+ON_SCALAR = ((0, 1),)
 GATE_STEP = 5
 GATE_COL = (0, 104)
 
@@ -45,8 +50,8 @@ def tile_moe_wsel_b_relu2_p_kernel(
         list1 = keep.tile([P, G * H // 16], U16, name="list1")
         list2 = keep.tile([P, G * N // 16], U16, name="list2")
         w1_all = [keep.tile([P, COLS], I32, name=f"w1_all{s}", align_bytes=64) for s in range(PASSES)]
-        w2_all = keep.tile([P, COLS], I32, name="w2_all", align_bytes=64)
-        x_w = [keep.tile([P, T], I32, name=f"x_w{s}", align_bytes=64) for s in range(PASSES)]
+        w2_all = keep.tile([P, COLS], I32, name="w2_all", tag="w2_all", align_bytes=64)
+        x_w = keep.tile([P, PASSES * T], I32, name="x_w", align_bytes=64)
         w1s_all = keep.tile([P, COLS], U8, name="w1s_all", align_bytes=64)
         w2s_all = keep.tile([P, COLS], U8, name="w2s_all", align_bytes=64)
         x_s = keep.tile([P, PASSES * T], U8, name="x_s", align_bytes=64)
@@ -54,35 +59,34 @@ def tile_moe_wsel_b_relu2_p_kernel(
         gate_cols = keep.tile([P, P], F32, name="gate_cols")
         ident = keep.tile([P, P], F32, name="ident")
 
-        nc.vector.memset(w2s_all[:].bitcast(I32), 0)
+        nc.gpsimd.memset(w2s_all[:].bitcast(I32), 0)
         nc.vector.memset(w1s_all[:].bitcast(I32), 0)
         nc.vector.memset(x_s[:].bitcast(I32), 0)
         make_identity(nc, ident[:])
 
-        for q in range(4):
-            nc.scalar.dma_start(
-                w2s_all[32 * q + W2_ROW : 32 * q + W2_ROW + 4, :].bitcast(I32),
-                w2_scales[0, 4 * q : 4 * q + 4, :].bitcast(I32),
-            )
         nc.sync.dma_start(list2[:], offs2)
         nc.sync.dma_start(list1[:], offs)
-        nc.sync.dma_start(w1_all[0][:], words(w1_words[0]))
+        nc.sync.dma_start(x_w[:, 0:T], words(x_words[0]))
+        for j in range(4):
+            nc.sync.dma_start(
+                w2s_all[W2_ROW + j : P : 32, :].bitcast(I32), w2_scales[0, j:16:4, :].bitcast(I32)
+            )
         for q in range(4):
             nc.sync.dma_start(
                 w1s_all[32 * q : 32 * q + 4 * PASSES, :].bitcast(I32),
                 w1_scales[:, 4 * q : 4 * q + 4, :].bitcast(I32),
             )
+        nc.sync.dma_start(w1_all[0][:], words(w1_words[0]))
+        for j in range(4):
+            nc.sync.dma_start(
+                x_s[X_ROW + j : P : 32, :].bitcast(I32).rearrange("q (s t) -> q s t", s=PASSES),
+                x_scales[:, j:16:4, :].rearrange("s q t -> q s t").bitcast(I32),
+            )
+        nc.sync.dma_start(w1_all[1][:], words(w1_words[1]))
         nc.sync.dma_start(
             gate_rows[:], gate.rearrange("r p (a c) -> (r p a) c", c=P)[0 : GATE_STEP * P : GATE_STEP, :]
         )
-        nc.sync.dma_start(w1_all[1][:], words(w1_words[1]))
-        for q in range(4):
-            nc.sync.dma_start(
-                x_s[32 * q + X_ROW : 32 * q + X_ROW + 4, :].bitcast(I32).rearrange("j (s t) -> j s t", s=PASSES),
-                x_scales[:, 4 * q : 4 * q + 4, :].rearrange("s j t -> j s t").bitcast(I32),
-            )
-        for s in range(PASSES):
-            nc.sync.dma_start(x_w[s][:], words(x_words[s]))
+        nc.sync.dma_start(x_w[:, T : 2 * T], words(x_words[1]))
         nc.sync.dma_start(w2_all[:], words(w2_words[0]))
 
         gate_t = bank(4)
@@ -100,16 +104,16 @@ def tile_moe_wsel_b_relu2_p_kernel(
             return dst
 
         nc.vector.tensor_copy(w2_s[:], w2s_all[:].indirect(list2[:]))
+        nc.vector.tensor_copy(w1_s[:], w1s_all[:].indirect(list1[:]))
         for r in range(G):
             w1_w[0, r] = gather_words(w1_all[0], list1, r, f"w1_w0{r}")
-        nc.vector.tensor_copy(w1_s[:], w1s_all[:].indirect(list1[:]))
         for r in range(G):
             w1_w[1, r] = gather_words(w1_all[1], list1, r, f"w1_w1{r}")
 
         def first_product(acc, tt, r, s):
             nc.tensor.matmul_mx(
                 out=acc[:],
-                lhsT=x_w[s][:, tt * P : (tt + 1) * P].bitcast(FP8X4),
+                lhsT=x_w[:, s * T + tt * P : s * T + (tt + 1) * P].bitcast(FP8X4),
                 lhsT_scale=x_s[X_ROW:P, s * T + tt * P : s * T + (tt + 1) * P],
                 rhs=w1_w[s, r][:].bitcast(FP8X4),
                 rhs_scale=w1_s[4 * s : P, r * H : (r + 1) * H],
@@ -117,30 +121,43 @@ def tile_moe_wsel_b_relu2_p_kernel(
                 stop=(s == PASSES - 1),
             )
 
-        units = [(tt, r) for tt in range(TILES) for r in range(G)]
+        units = [(0, 0), (1, 0), (0, 1), (1, 1), (2, 0), (2, 1), (3, 0), (3, 1)]
         pre = {u: bank(b) for b, u in enumerate(units[:AHEAD])}
-        for tt, r in units[:AHEAD]:
-            for s in range(PASSES):
+        for s in range(PASSES):
+            for tt, r in units[:AHEAD]:
                 first_product(pre[tt, r], tt, r, s)
 
-        hidden = {}
+        h_early = keep.tile([P, EARLY * H], BF16, name="h_early", align_bytes=64)
+        hidden = {u: h_early[:, i * H : (i + 1) * H] for i, u in enumerate(units[:EARLY])}
 
-        def activate(tt, r):
-            pos = keep.tile([P, H], F32, name=f"pos{tt}{r}", tag=f"pos{tt}{r}", align_bytes=64)
+        positive = {}
+
+        def rectify(tt, r):
+            pos = keep.tile([P, H], F32, name=f"pos{tt}{r}", tag=f"pos{units.index((tt, r)) % 3}")
             nc.scalar.activation(
                 pos[:].rearrange("t (u q e) -> t u q e", u=2, e=2),
                 pre[tt, r][:].rearrange("t (q u e) -> t u q e", u=2, e=2),
                 RELU,
             )
-            later = units.index((tt, r)) + AHEAD
-            if later < len(units):
-                pre[units[later]] = bank(later % AHEAD)
+            later = units.index((tt, r)) + PACE
+            if AHEAD <= later < len(units):
+                pre[units[later]] = bank(AHEAD - PACE + later % PACE)
                 for s in range(PASSES):
                     first_product(pre[units[later]], *units[later], s)
-            h = ring.tile([P, H], BF16, name="h", align_bytes=64)
+            positive[tt, r] = pos
+            if (tt, r) in ON_SCALAR:
+                activate(tt, r)
+
+        def activate(tt, r):
+            pos = positive[tt, r]
+            h = hidden[tt, r]
             col = GATE_COL[r] + tt
-            nc.vector.scalar_tensor_tensor(h[:], pos[:], gate_cols[:, col : col + 1], pos[:], MULT, MULT)
-            hidden[tt, r] = h
+            if (tt, r) in ON_SCALAR:
+                sq = keep.tile([P, H], F32, name=f"sq{tt}{r}")
+                nc.scalar.activation(sq[:], pos[:], SQUARE)
+                nc.scalar.activation(h, sq[:], COPY, scale=gate_cols[:, col : col + 1])
+            else:
+                nc.vector.scalar_tensor_tensor(h, pos[:], gate_cols[:, col : col + 1], pos[:], MULT, MULT)
 
         codes = {}
 
@@ -151,17 +168,21 @@ def tile_moe_wsel_b_relu2_p_kernel(
                 for u in range(2):
                     nc.tensor.transpose(
                         turned[:, (2 * i + u) * P : (2 * i + u + 1) * P],
-                        hidden[tt, r][:].bitcast(F32)[:, u * P : (u + 1) * P],
+                        hidden[tt, r].bitcast(F32)[:, u * P : (u + 1) * P],
                         ident[:],
                     )
-            h_t = ring.tile([P, n * P * 4], BF16, name="h_t", align_bytes=64)
+            if tt == 0:
+                h_t = h_late[:, (len(units) - EARLY) * H :]
+            else:
+                h_t_tile = ring.tile([P, n * P * 4], BF16, name="h_t", align_bytes=64)
+                h_t = h_t_tile[:]
             nc.scalar.copy(
-                h_t[:].bitcast(F32).rearrange("q (r t u) -> q r t u", r=n, u=2),
+                h_t.bitcast(F32).rearrange("q (r t u) -> q r t u", r=n, u=2),
                 turned[:, 0 : 2 * n * P].rearrange("q (r u t) -> q r t u", r=n, u=2),
             )
             h_w = keep.tile([P, n * P], U32, name=f"h_w{tt}{experts[0]}", align_bytes=64)
             h_s = keep.tile([P, n * P], U8, name=f"h_s{tt}{experts[0]}", align_bytes=64)
-            nc.vector.quantize_mx(out=h_w[:].bitcast(FP8X4), scales=h_s[:], in_=h_t[:])
+            nc.vector.quantize_mx(out=h_w[:].bitcast(FP8X4), scales=h_s[:], in_=h_t)
             for i, r in enumerate(experts):
                 codes[tt, r] = (h_w[:, i * P : (i + 1) * P], h_s[:, i * P : (i + 1) * P])
 
@@ -185,19 +206,26 @@ def tile_moe_wsel_b_relu2_p_kernel(
                 for r in range(G):
                     second_pass(acc[:, j * P : (j + 1) * P], tt, j, r)
             res = ring.tile([P, N], F32, name="res")
-            nc.scalar.copy(res[:], acc[:])
+            if tt == 1:
+                nc.vector.tensor_copy(res[:], acc[:])
+            else:
+                nc.scalar.copy(res[:], acc[:])
             nc.sync.dma_start(
                 out_view[:, :, tt * P : (tt + 1) * P], res[:].rearrange("p (j t) -> p j t", t=P)
             )
 
         last = TILES - 1
+        for u in units:
+            rectify(*u)
         activate(0, 0)
-        activate(0, 1)
         activate(1, 0)
-        w2_w[0] = gather_words(w2_all, list2, 0, "pos10")
-        turn(0, range(G), 4)
         activate(1, 1)
-        w2_w[1] = gather_words(w2_all, list2, 1, "pos11")
+        for r in range(G):
+            w2_w[r] = gather_words(w2_all, list2, r, f"w2_w{r}")
+        h_late = keep.tile([P, (len(units) - EARLY + G) * H], BF16, name="h_late", tag="w2_all", align_bytes=64)
+        for i, u in enumerate(units[EARLY:]):
+            hidden[u] = h_late[:, i * H : (i + 1) * H]
+        turn(0, range(G), 4)
         activate(2, 0)
         turn(1, range(G), 5)
         second_product(0)
@@ -207,8 +235,8 @@ def tile_moe_wsel_b_relu2_p_kernel(
         turn(2, range(G), 4)
         activate(last, 1)
         turn(last, [0], 5)
-        second_product(2)
         turn(last, [1], 4)
+        second_product(2)
         accs = [bank(j) for j in range(N // P)]
         for r in range(G):
             for j in range(N // P):

@@ -22,14 +22,9 @@ P = 128
 PASSES = K // 512
 TILES = T // P
 COLS = E * H
+CUTS = (512, 1408)
 X_ROW = 8
 W2_ROW = 12
-AHEAD = 4
-PACE = 2
-EARLY = 4
-ON_SCALAR = ((0, 1),)
-GATE_STEP = 5
-GATE_COL = (0, 104)
 
 
 def tile_moe_wsel_b_relu2_p_kernel(
@@ -38,7 +33,7 @@ def tile_moe_wsel_b_relu2_p_kernel(
     nc = tc.nc
     with ExitStack() as ctx:
         keep = ctx.enter_context(tc.tile_pool(name="keep", bufs=1))
-        ring = ctx.enter_context(tc.tile_pool(name="ring", bufs=4))
+        reuse = ctx.enter_context(tc.tile_pool(name="reuse", bufs=1))
         psum = ctx.enter_context(tc.psum_pool(name="psum", bufs=1))
 
         def words(dram):
@@ -50,33 +45,44 @@ def tile_moe_wsel_b_relu2_p_kernel(
         list1 = keep.tile([P, G * H // 16], U16, name="list1")
         list2 = keep.tile([P, G * N // 16], U16, name="list2")
         w1_all = [keep.tile([P, COLS], I32, name=f"w1_all{s}", align_bytes=64) for s in range(PASSES)]
-        w2_all = keep.tile([P, COLS], I32, name="w2_all", tag="w2_all", align_bytes=64)
-        x_w = keep.tile([P, PASSES * T], I32, name="x_w", align_bytes=64)
+        w2_all = reuse.tile([P, COLS], I32, name="w2_all", align_bytes=64, offset=0)
+        x_w = [keep.tile([P, T], I32, name=f"x_w{s}", align_bytes=64) for s in range(PASSES)]
         w1s_all = keep.tile([P, COLS], U8, name="w1s_all", align_bytes=64)
         w2s_all = keep.tile([P, COLS], U8, name="w2s_all", align_bytes=64)
+        w1_s = keep.tile([P, G * H], U8, name="w1_s", align_bytes=64)
+        w2s_picked = keep.tile([P, G * N], U8, name="w2s_picked", align_bytes=64)
+        w2_s = keep.tile([P, G * N], U8, name="w2_s", align_bytes=64)
         x_s = keep.tile([P, PASSES * T], U8, name="x_s", align_bytes=64)
         gate_rows = keep.tile([P, P], F32, name="gate_rows")
-        gate_cols = keep.tile([P, P], F32, name="gate_cols")
+        gate_cols = keep.tile([P, G * TILES], F32, name="gate_cols")
         ident = keep.tile([P, P], F32, name="ident")
 
         nc.gpsimd.memset(w2s_all[:].bitcast(I32), 0)
         nc.vector.memset(w1s_all[:].bitcast(I32), 0)
         nc.vector.memset(x_s[:].bitcast(I32), 0)
+        nc.gpsimd.memset(gate_rows[:], 0.0)
+        nc.gpsimd.memset(w2_s[:].bitcast(I32), 0)
         make_identity(nc, ident[:])
 
+        def load_w1_scales(rows):
+            for s, j in rows:
+                nc.sync.dma_start(
+                    w1s_all[4 * s + j : P : 32, :].bitcast(I32), w1_scales[s, j:16:4, :].bitcast(I32)
+                )
+
+        def load_w1_piece(lo, hi):
+            nc.sync.dma_start(w1_all[0][:, lo:hi], words(w1_words[0])[:, lo:hi])
+
+        scale_rows = [(s, j) for s in range(PASSES) for j in range(4)]
         nc.sync.dma_start(list2[:], offs2)
+        load_w1_piece(0, CUTS[0])
+        nc.sync.dma_start(w2s_all[0:P:8, :].bitcast(I32), w2_scales[0].bitcast(I32))
         nc.sync.dma_start(list1[:], offs)
-        nc.sync.dma_start(x_w[:, 0:T], words(x_words[0]))
-        for j in range(4):
-            nc.sync.dma_start(
-                w2s_all[W2_ROW + j : P : 32, :].bitcast(I32), w2_scales[0, j:16:4, :].bitcast(I32)
-            )
-        for q in range(4):
-            nc.sync.dma_start(
-                w1s_all[32 * q : 32 * q + 4 * PASSES, :].bitcast(I32),
-                w1_scales[:, 4 * q : 4 * q + 4, :].bitcast(I32),
-            )
-        nc.sync.dma_start(w1_all[0][:], words(w1_words[0]))
+        load_w1_scales(scale_rows[:3])
+        load_w1_piece(CUTS[0], CUTS[1])
+        load_w1_scales(scale_rows[3:])
+        load_w1_piece(CUTS[1], COLS)
+        nc.sync.dma_start(x_w[0][:], words(x_words[0]))
         for j in range(4):
             nc.sync.dma_start(
                 x_s[X_ROW + j : P : 32, :].bitcast(I32).rearrange("q (s t) -> q s t", s=PASSES),
@@ -84,36 +90,44 @@ def tile_moe_wsel_b_relu2_p_kernel(
             )
         nc.sync.dma_start(w1_all[1][:], words(w1_words[1]))
         nc.sync.dma_start(
-            gate_rows[:], gate.rearrange("r p (a c) -> (r p a) c", c=P)[0 : GATE_STEP * P : GATE_STEP, :]
+            gate_rows[0 : G * TILES, :], gate[:, 0, :].rearrange("r (a c) -> r a c", c=P)
         )
-        nc.sync.dma_start(x_w[:, T : 2 * T], words(x_words[1]))
+
+        nc.vector.tensor_copy(w2s_picked[:], w2s_all[:].indirect(list2[:]))
+        for j in range(4):
+            nc.sync.dma_start(
+                w2_s[W2_ROW + j : P : 32, :].bitcast(I32), w2s_picked[8 * j : P : 32, :].bitcast(I32)
+            )
+        nc.sync.dma_start(x_w[1][:], words(x_words[1]))
         nc.sync.dma_start(w2_all[:], words(w2_words[0]))
 
-        gate_t = bank(4)
+        gate_t = bank(7)
         nc.tensor.transpose(gate_t[:, 0:P], gate_rows[:], ident[:])
-        nc.scalar.copy(gate_cols[:], gate_t[:, 0:P])
+        nc.scalar.copy(gate_cols[:], gate_t[:, 0 : G * TILES])
 
-        w1_w = {}
-        w2_w = {}
-        w1_s = keep.tile([P, G * H], U8, name="w1_s", align_bytes=64)
-        w2_s = keep.tile([P, G * N], U8, name="w2_s", align_bytes=64)
-
-        def gather_words(src, lst, r, tag):
-            dst = keep.tile([P, 512], U32, name=f"picked_{tag}", tag=tag, align_bytes=64)
+        def gather_words(src, lst, r, name):
+            dst = keep.tile([P, 512], U32, name=name, align_bytes=64)
             nc.vector.tensor_copy(dst[:], src[:].bitcast(U32).indirect(lst[:, r * 32 : (r + 1) * 32]))
             return dst
 
-        nc.vector.tensor_copy(w2_s[:], w2s_all[:].indirect(list2[:]))
         nc.vector.tensor_copy(w1_s[:], w1s_all[:].indirect(list1[:]))
-        for r in range(G):
-            w1_w[0, r] = gather_words(w1_all[0], list1, r, f"w1_w0{r}")
-        for r in range(G):
-            w1_w[1, r] = gather_words(w1_all[1], list1, r, f"w1_w1{r}")
+        w1_w = {}
+        for s in range(PASSES):
+            for r in range(G):
+                w1_w[s, r] = gather_words(w1_all[s], list1, r, f"w1_w{s}{r}")
 
-        def first_product(acc, tt, r, s):
+        units = [(0, 0), (1, 0), (0, 1), (1, 1), (2, 0), (2, 1), (3, 0), (3, 1)]
+        pre = {}
+        pos = {}
+        sq = {}
+        hidden = {}
+        codes = {}
+
+        def first_pass(i, s):
+            tt, r = units[i]
             nc.tensor.matmul_mx(
-                out=acc[:],
-                lhsT=x_w[:, s * T + tt * P : s * T + (tt + 1) * P].bitcast(FP8X4),
+                out=pre[i][:],
+                lhsT=x_w[s][:, tt * P : (tt + 1) * P].bitcast(FP8X4),
                 lhsT_scale=x_s[X_ROW:P, s * T + tt * P : s * T + (tt + 1) * P],
                 rhs=w1_w[s, r][:].bitcast(FP8X4),
                 rhs_scale=w1_s[4 * s : P, r * H : (r + 1) * H],
@@ -121,135 +135,153 @@ def tile_moe_wsel_b_relu2_p_kernel(
                 stop=(s == PASSES - 1),
             )
 
-        units = [(0, 0), (1, 0), (0, 1), (1, 1), (2, 0), (2, 1), (3, 0), (3, 1)]
-        pre = {u: bank(b) for b, u in enumerate(units[:AHEAD])}
-        for s in range(PASSES):
-            for tt, r in units[:AHEAD]:
-                first_product(pre[tt, r], tt, r, s)
+        def first_product(i, b):
+            pre[i] = bank(b)
+            for s in range(PASSES):
+                first_pass(i, s)
 
-        h_early = keep.tile([P, EARLY * H], BF16, name="h_early", align_bytes=64)
-        hidden = {u: h_early[:, i * H : (i + 1) * H] for i, u in enumerate(units[:EARLY])}
-
-        positive = {}
-
-        def rectify(tt, r):
-            pos = keep.tile([P, H], F32, name=f"pos{tt}{r}", tag=f"pos{units.index((tt, r)) % 3}")
+        def rectify(i):
+            pos[i] = keep.tile([P, H], F32, name=f"pos{i}")
             nc.scalar.activation(
-                pos[:].rearrange("t (u q e) -> t u q e", u=2, e=2),
-                pre[tt, r][:].rearrange("t (q u e) -> t u q e", u=2, e=2),
+                pos[i][:].rearrange("t (u q e) -> t u q e", u=2, e=2),
+                pre[i][:].rearrange("t (q u e) -> t u q e", u=2, e=2),
                 RELU,
             )
-            later = units.index((tt, r)) + PACE
-            if AHEAD <= later < len(units):
-                pre[units[later]] = bank(AHEAD - PACE + later % PACE)
-                for s in range(PASSES):
-                    first_product(pre[units[later]], *units[later], s)
-            positive[tt, r] = pos
-            if (tt, r) in ON_SCALAR:
-                activate(tt, r)
 
-        def activate(tt, r):
-            pos = positive[tt, r]
-            h = hidden[tt, r]
-            col = GATE_COL[r] + tt
-            if (tt, r) in ON_SCALAR:
-                sq = keep.tile([P, H], F32, name=f"sq{tt}{r}")
-                nc.scalar.activation(sq[:], pos[:], SQUARE)
-                nc.scalar.activation(h, sq[:], COPY, scale=gate_cols[:, col : col + 1])
-            else:
-                nc.vector.scalar_tensor_tensor(h, pos[:], gate_cols[:, col : col + 1], pos[:], MULT, MULT)
+        def gate_col(i):
+            tt, r = units[i]
+            return gate_cols[:, r * TILES + tt : r * TILES + tt + 1]
 
-        codes = {}
+        def weigh_on_vector(i, h):
+            hidden[i] = h
+            nc.vector.scalar_tensor_tensor(h[:], pos[i][:], gate_col(i), pos[i][:], MULT, MULT)
 
-        def turn(tt, experts, b):
-            n = len(experts)
+        def square(i):
+            sq[i] = keep.tile([P, H], F32, name=f"sq{i}")
+            nc.scalar.activation(sq[i][:], pos[i][:], SQUARE)
+
+        def scale_on_scalar(i, h):
+            hidden[i] = h
+            nc.scalar.activation(h[:], sq[i][:], COPY, scale=gate_col(i))
+
+        def late(shape, dtype, name, slot):
+            return reuse.tile(shape, dtype, name=name, align_bytes=64, offset=1024 * slot)
+
+        def turned_tile(n, name):
+            return keep.tile([P, n * H], BF16, name=name, align_bytes=64)
+
+        def h_tile(i):
+            return keep.tile([P, H], BF16, name=f"h{i}", align_bytes=64)
+
+        def turn(group, b, copy, h_t):
+            n = len(group)
             turned = bank(b)
-            for i, r in enumerate(experts):
+            for m, i in enumerate(group):
                 for u in range(2):
                     nc.tensor.transpose(
-                        turned[:, (2 * i + u) * P : (2 * i + u + 1) * P],
-                        hidden[tt, r].bitcast(F32)[:, u * P : (u + 1) * P],
+                        turned[:, (2 * m + u) * P : (2 * m + u + 1) * P],
+                        hidden[i][:].bitcast(F32)[:, u * P : (u + 1) * P],
                         ident[:],
                     )
-            if tt == 0:
-                h_t = h_late[:, (len(units) - EARLY) * H :]
-            else:
-                h_t_tile = ring.tile([P, n * P * 4], BF16, name="h_t", align_bytes=64)
-                h_t = h_t_tile[:]
-            nc.scalar.copy(
-                h_t.bitcast(F32).rearrange("q (r t u) -> q r t u", r=n, u=2),
-                turned[:, 0 : 2 * n * P].rearrange("q (r u t) -> q r t u", r=n, u=2),
+            copy(
+                h_t[:].bitcast(F32).rearrange("q (m t u) -> q m t u", m=n, u=2),
+                turned[:, 0 : 2 * n * P].rearrange("q (m u t) -> q m t u", m=n, u=2),
             )
-            h_w = keep.tile([P, n * P], U32, name=f"h_w{tt}{experts[0]}", align_bytes=64)
-            h_s = keep.tile([P, n * P], U8, name=f"h_s{tt}{experts[0]}", align_bytes=64)
-            nc.vector.quantize_mx(out=h_w[:].bitcast(FP8X4), scales=h_s[:], in_=h_t)
-            for i, r in enumerate(experts):
-                codes[tt, r] = (h_w[:, i * P : (i + 1) * P], h_s[:, i * P : (i + 1) * P])
+            return h_t
+
+        def quantise(group, h_t, h_w):
+            n = len(group)
+            h_s = keep.tile([P, n * P], U8, name=f"h_s{group[0]}", align_bytes=64)
+            nc.vector.quantize_mx(out=h_w[:].bitcast(FP8X4), scales=h_s[:], in_=h_t[:])
+            codes[group] = (h_w, h_s)
 
         out_view = out.rearrange("(j p) t -> p j t", p=P)
 
-        def second_pass(acc, tt, j, r):
-            h_w, h_s = codes[tt, r]
+        def second_pass(acc, j, r, group, lo, hi):
+            h_w, h_s = codes[group]
             nc.tensor.matmul_mx(
                 out=acc,
                 lhsT=w2_w[r][:, j * P : (j + 1) * P].bitcast(FP8X4),
                 lhsT_scale=w2_s[W2_ROW:P, r * N + j * P : r * N + (j + 1) * P],
-                rhs=h_w.bitcast(FP8X4),
-                rhs_scale=h_s,
+                rhs=h_w[:, lo:hi].bitcast(FP8X4),
+                rhs_scale=h_s[:, lo:hi],
                 start=(r == 0),
                 stop=(r == G - 1),
             )
 
-        def second_product(tt):
-            acc = bank(6 + tt % 2)
+        for i in range(4):
+            pre[i] = bank(i)
+        for s in range(PASSES):
+            for i in range(4):
+                first_pass(i, s)
+
+        rectify(0)
+        rectify(1)
+        first_product(4, 1)
+        weigh_on_vector(0, h_tile(0))
+        rectify(2)
+        weigh_on_vector(1, h_tile(1))
+        rectify(3)
+        first_product(5, 3)
+        weigh_on_vector(2, h_tile(2))
+        square(3)
+        rectify(4)
+        first_product(6, 1)
+        h_t0 = turn((0, 2), 4, nc.scalar.copy, late([P, G * H], BF16, "h_t0", 12))
+        first_product(7, 4)
+        scale_on_scalar(3, h_tile(3))
+        rectify(5)
+        h_t1 = turn((1, 3), 5, nc.scalar.copy, late([P, G * H], BF16, "h_t1", 14))
+        rectify(6)
+        rectify(7)
+        w2_w = [gather_words(w2_all, list2, r, f"w2_w{r}") for r in range(G)]
+
+        def codes_tile(n, name):
+            return keep.tile([P, n * P], U32, name=name, align_bytes=64)
+
+        def second_product(group, b):
+            acc = bank(b)
             for j in range(N // P):
                 for r in range(G):
-                    second_pass(acc[:, j * P : (j + 1) * P], tt, j, r)
-            res = ring.tile([P, N], F32, name="res")
-            if tt == 1:
-                nc.vector.tensor_copy(res[:], acc[:])
-            else:
-                nc.scalar.copy(res[:], acc[:])
+                    second_pass(acc[:, j * P : (j + 1) * P], j, r, group, r * P, (r + 1) * P)
+            return acc
+
+        def store(tt, acc, copy):
+            res = keep.tile([P, N], F32, name=f"res{tt}")
+            copy(res[:], acc[:])
             nc.sync.dma_start(
                 out_view[:, :, tt * P : (tt + 1) * P], res[:].rearrange("p (j t) -> p j t", t=P)
             )
 
-        last = TILES - 1
-        for u in units:
-            rectify(*u)
-        activate(0, 0)
-        activate(1, 0)
-        activate(1, 1)
+        quantise((0, 2), h_t0, late([P, G * P], U32, "h_w0", 0))
+        acc0 = second_product((0, 2), 6)
+        weigh_on_vector(4, late([P, H], BF16, "h4", 12))
+        weigh_on_vector(5, late([P, H], BF16, "h5", 13))
+        quantise((1, 3), h_t1, late([P, G * P], U32, "h_w1", 1))
+        weigh_on_vector(6, late([P, H], BF16, "h6", 14))
+        weigh_on_vector(7, late([P, H], BF16, "h7", 15))
+        h_t2 = turn((4, 5), 0, nc.scalar.copy, turned_tile(G, "h_t2"))
+        acc1 = second_product((1, 3), 7)
+        store(0, acc0, nc.scalar.copy)
+        quantise((4, 5), h_t2, codes_tile(G, "h_w2"))
+        store(1, acc1, nc.vector.tensor_copy)
+        acc2 = second_product((4, 5), 3)
+        accs = [bank(b) for b in (1, 4, 6, 0)]
         for r in range(G):
-            w2_w[r] = gather_words(w2_all, list2, r, f"w2_w{r}")
-        h_late = keep.tile([P, (len(units) - EARLY + G) * H], BF16, name="h_late", tag="w2_all", align_bytes=64)
-        for i, u in enumerate(units[EARLY:]):
-            hidden[u] = h_late[:, i * H : (i + 1) * H]
-        turn(0, range(G), 4)
-        activate(2, 0)
-        turn(1, range(G), 5)
-        second_product(0)
-        activate(2, 1)
-        activate(last, 0)
-        second_product(1)
-        turn(2, range(G), 4)
-        activate(last, 1)
-        turn(last, [0], 5)
-        turn(last, [1], 4)
-        second_product(2)
-        accs = [bank(j) for j in range(N // P)]
-        for r in range(G):
+            group = (6 + r,)
+            quantise(group, turn(group, (2, 5)[r], nc.scalar.copy, turned_tile(1, f"h_t3{r}")), codes_tile(1, f"h_w3{r}"))
             for j in range(N // P):
-                second_pass(accs[j][:, 0:P], last, j, r)
+                second_pass(accs[j][:, 0:P], j, r, group, 0, P)
+        store(2, acc2, nc.scalar.copy)
         halves = [keep.tile([P, 2 * P], F32, name=f"half{i}") for i in range(2)]
         for j in range(N // P):
             dst = halves[j // 2][:, (j % 2) * P : (j % 2 + 1) * P]
-            if j % 2 == 0:
-                nc.vector.tensor_copy(dst, accs[j][:, 0:P])
-            else:
+            if j == 2:
                 nc.scalar.copy(dst, accs[j][:, 0:P])
+            else:
+                nc.vector.tensor_copy(dst, accs[j][:, 0:P])
             if j % 2 == 1:
                 nc.sync.dma_start(
-                    out_view[:, j - 1 : j + 1, last * P : (last + 1) * P],
+                    out_view[:, j - 1 : j + 1, 3 * P : 4 * P],
                     halves[j // 2][:].rearrange("p (j t) -> p j t", t=P),
                 )

@@ -220,20 +220,21 @@ def tile_moe_wsel_b_relu2_p_kernel(
         first_product(4, 1)
         weigh_on_vector(0, h_tile(0))
         rectify(2)
+        first_product(5, 2)
         weigh_on_vector(1, h_tile(1))
         rectify(3)
-        first_product(5, 3)
         weigh_on_vector(2, h_tile(2))
-        square(3)
         rectify(4)
         first_product(6, 1)
+        weigh_on_vector(3, h_tile(3))
+        rectify(5)
         h_t0 = turn((0, 2), 4, nc.scalar.copy, late([P, G * H], BF16, "h_t0", 12))
         first_product(7, 4)
-        scale_on_scalar(3, h_tile(3))
-        rectify(5)
-        h_t1 = turn((1, 3), 5, nc.scalar.copy, late([P, G * H], BF16, "h_t1", 14))
         rectify(6)
+        h_t1 = turn((1, 3), 5, nc.scalar.copy, late([P, G * H], BF16, "h_t1", 14))
+        square(6)
         rectify(7)
+        scale_on_scalar(6, h_tile(6))
         w2_w = [gather_words(w2_all, list2, r, f"w2_w{r}") for r in range(G)]
 
         def codes_tile(n, name):
@@ -258,18 +259,17 @@ def tile_moe_wsel_b_relu2_p_kernel(
         weigh_on_vector(4, late([P, H], BF16, "h4", 12))
         weigh_on_vector(5, late([P, H], BF16, "h5", 13))
         quantise((1, 3), h_t1, late([P, G * P], U32, "h_w1", 1))
-        weigh_on_vector(6, late([P, H], BF16, "h6", 14))
         weigh_on_vector(7, late([P, H], BF16, "h7", 15))
         h_t2 = turn((4, 5), 0, nc.scalar.copy, turned_tile(G, "h_t2"))
         acc1 = second_product((1, 3), 7)
         store(0, acc0, nc.scalar.copy)
         quantise((4, 5), h_t2, codes_tile(G, "h_w2"))
         store(1, acc1, nc.vector.tensor_copy)
-        acc2 = second_product((4, 5), 3)
+        acc2 = second_product((4, 5), 2)
         accs = [bank(b) for b in (1, 4, 6, 0)]
         for r in range(G):
             group = (6 + r,)
-            quantise(group, turn(group, (2, 5)[r], nc.scalar.copy, turned_tile(1, f"h_t3{r}")), codes_tile(1, f"h_w3{r}"))
+            quantise(group, turn(group, (3, 5)[r], nc.scalar.copy, turned_tile(1, f"h_t3{r}")), codes_tile(1, f"h_w3{r}"))
             for j in range(N // P):
                 second_pass(accs[j][:, 0:P], j, r, group, 0, P)
         store(2, acc2, nc.scalar.copy)

@@ -22,7 +22,6 @@ P = 128
 PASSES = K // 512
 TILES = T // P
 COLS = E * H
-CUTS = (512, 1408)
 X_ROW = 8
 W2_ROW = 12
 
@@ -64,42 +63,33 @@ def tile_moe_wsel_b_relu2_p_kernel(
         nc.gpsimd.memset(w2_s[:].bitcast(I32), 0)
         make_identity(nc, ident[:])
 
-        def load_w1_scales(rows):
-            for s, j in rows:
-                nc.sync.dma_start(
-                    w1s_all[4 * s + j : P : 32, :].bitcast(I32), w1_scales[s, j:16:4, :].bitcast(I32)
-                )
-
-        def load_w1_piece(lo, hi):
-            nc.sync.dma_start(w1_all[0][:, lo:hi], words(w1_words[0])[:, lo:hi])
-
-        scale_rows = [(s, j) for s in range(PASSES) for j in range(4)]
         nc.sync.dma_start(list2[:], offs2)
-        load_w1_piece(0, CUTS[0])
-        nc.sync.dma_start(w2s_all[0:P:8, :].bitcast(I32), w2_scales[0].bitcast(I32))
         nc.sync.dma_start(list1[:], offs)
-        load_w1_scales(scale_rows[:3])
-        load_w1_piece(CUTS[0], CUTS[1])
-        load_w1_scales(scale_rows[3:])
-        load_w1_piece(CUTS[1], COLS)
+        nc.sync.dma_start(w2s_all[0:P:8, :].bitcast(I32), w2_scales[0].bitcast(I32))
+        for q in range(4):
+            nc.sync.dma_start(
+                w1s_all[32 * q : 32 * q + 4 * PASSES, :].bitcast(I32),
+                w1_scales[:, 4 * q : 4 * q + 4, :].bitcast(I32),
+            )
+        nc.sync.dma_start(w1_all[0][:], words(w1_words[0]))
         nc.sync.dma_start(x_w[0][:], words(x_words[0]))
         for j in range(4):
             nc.sync.dma_start(
                 x_s[X_ROW + j : P : 32, :].bitcast(I32).rearrange("q (s t) -> q s t", s=PASSES),
                 x_scales[:, j:16:4, :].rearrange("s q t -> q s t").bitcast(I32),
             )
-        nc.sync.dma_start(w1_all[1][:], words(w1_words[1]))
         nc.sync.dma_start(
             gate_rows[0 : G * TILES, :], gate[:, 0, :].rearrange("r (a c) -> r a c", c=P)
         )
+        nc.sync.dma_start(w1_all[1][:], words(w1_words[1]))
+        nc.sync.dma_start(x_w[1][:], words(x_words[1]))
+        nc.sync.dma_start(w2_all[:], words(w2_words[0]))
 
         nc.vector.tensor_copy(w2s_picked[:], w2s_all[:].indirect(list2[:]))
         for j in range(4):
             nc.sync.dma_start(
                 w2_s[W2_ROW + j : P : 32, :].bitcast(I32), w2s_picked[8 * j : P : 32, :].bitcast(I32)
             )
-        nc.sync.dma_start(x_w[1][:], words(x_words[1]))
-        nc.sync.dma_start(w2_all[:], words(w2_words[0]))
 
         gate_t = bank(7)
         nc.tensor.transpose(gate_t[:, 0:P], gate_rows[:], ident[:])

@@ -44,12 +44,12 @@ def tile_moe_wsel_b_relu2_p_kernel(
         list1 = keep.tile([P, G * H // 16], U16, name="list1")
         list2 = keep.tile([P, G * N // 16], U16, name="list2")
         w1_all = [keep.tile([P, COLS], I32, name=f"w1_all{s}", align_bytes=64) for s in range(PASSES)]
-        w2_all = reuse.tile([P, COLS], I32, name="w2_all", align_bytes=64, offset=0)
+        w2_all = keep.tile([P, COLS], I32, name="w2_all", align_bytes=64)
         x_w = [keep.tile([P, T], I32, name=f"x_w{s}", align_bytes=64) for s in range(PASSES)]
         w1s_all = keep.tile([P, COLS], U8, name="w1s_all", align_bytes=64)
         w2s_all = keep.tile([P, COLS], U8, name="w2s_all", align_bytes=64)
         w1_s = keep.tile([P, G * H], U8, name="w1_s", align_bytes=64)
-        w2s_picked = keep.tile([P, G * N], U8, name="w2s_picked", align_bytes=64)
+        w2s_picked = reuse.tile([P, 3 * 1024], U8, name="w2s_picked", align_bytes=64, offset=32 * 1024)
         w2_s = keep.tile([P, G * N], U8, name="w2_s", align_bytes=64)
         x_s = keep.tile([P, PASSES * T], U8, name="x_s", align_bytes=64)
         gate_rows = keep.tile([P, P], F32, name="gate_rows")
@@ -65,30 +65,31 @@ def tile_moe_wsel_b_relu2_p_kernel(
 
         nc.sync.dma_start(list2[:], offs2)
         nc.sync.dma_start(list1[:], offs)
+        nc.sync.dma_start(x_w[0][:], words(x_words[0]))
         nc.sync.dma_start(w2s_all[0:P:8, :].bitcast(I32), w2_scales[0].bitcast(I32))
+        nc.sync.dma_start(
+            gate_rows[0 : G * TILES, :], gate[:, 0, :].rearrange("r (a c) -> r a c", c=P)
+        )
         for q in range(4):
             nc.sync.dma_start(
                 w1s_all[32 * q : 32 * q + 4 * PASSES, :].bitcast(I32),
                 w1_scales[:, 4 * q : 4 * q + 4, :].bitcast(I32),
             )
-        nc.sync.dma_start(w1_all[0][:], words(w1_words[0]))
-        nc.sync.dma_start(x_w[0][:], words(x_words[0]))
         for j in range(4):
             nc.sync.dma_start(
                 x_s[X_ROW + j : P : 32, :].bitcast(I32).rearrange("q (s t) -> q s t", s=PASSES),
                 x_scales[:, j:16:4, :].rearrange("s q t -> q s t").bitcast(I32),
             )
-        nc.sync.dma_start(
-            gate_rows[0 : G * TILES, :], gate[:, 0, :].rearrange("r (a c) -> r a c", c=P)
-        )
-        nc.sync.dma_start(w1_all[1][:], words(w1_words[1]))
+        for s in range(PASSES):
+            nc.sync.dma_start(w1_all[s][:], words(w1_words[s]))
         nc.sync.dma_start(x_w[1][:], words(x_words[1]))
         nc.sync.dma_start(w2_all[:], words(w2_words[0]))
 
-        nc.vector.tensor_copy(w2s_picked[:], w2s_all[:].indirect(list2[:]))
+        nc.vector.tensor_copy(w2s_picked[:, 0 : G * N], w2s_all[:].indirect(list2[:]))
         for j in range(4):
             nc.sync.dma_start(
-                w2_s[W2_ROW + j : P : 32, :].bitcast(I32), w2s_picked[8 * j : P : 32, :].bitcast(I32)
+                w2_s[W2_ROW + j : P : 32, :].bitcast(I32),
+                w2s_picked[8 * j : P : 32, 0 : G * N].bitcast(I32),
             )
 
         gate_t = bank(7)
@@ -131,7 +132,7 @@ def tile_moe_wsel_b_relu2_p_kernel(
                 first_pass(i, s)
 
         def rectify(i):
-            pos[i] = keep.tile([P, H], F32, name=f"pos{i}")
+            pos[i] = late([P, H], F32, f"pos{i}", 16 + 2 * i)
             nc.scalar.activation(
                 pos[i][:].rearrange("t (u q e) -> t u q e", u=2, e=2),
                 pre[i][:].rearrange("t (q u e) -> t u q e", u=2, e=2),
@@ -219,8 +220,8 @@ def tile_moe_wsel_b_relu2_p_kernel(
         weigh_on_vector(3, h_tile(3))
         rectify(5)
         h_t0 = turn((0, 2), 4, nc.scalar.copy, late([P, G * H], BF16, "h_t0", 12))
-        first_product(7, 4)
         rectify(6)
+        first_product(7, 1)
         h_t1 = turn((1, 3), 5, nc.scalar.copy, late([P, G * H], BF16, "h_t1", 14))
         square(6)
         rectify(7)
@@ -244,29 +245,31 @@ def tile_moe_wsel_b_relu2_p_kernel(
                 out_view[:, :, tt * P : (tt + 1) * P], res[:].rearrange("p (j t) -> p j t", t=P)
             )
 
-        quantise((0, 2), h_t0, late([P, G * P], U32, "h_w0", 0))
+        quantise((0, 2), h_t0, late([P, G * P], U32, "h_w0", 32))
         acc0 = second_product((0, 2), 6)
-        weigh_on_vector(4, late([P, H], BF16, "h4", 12))
-        weigh_on_vector(5, late([P, H], BF16, "h5", 13))
-        quantise((1, 3), h_t1, late([P, G * P], U32, "h_w1", 1))
-        weigh_on_vector(7, late([P, H], BF16, "h7", 15))
-        h_t2 = turn((4, 5), 0, nc.scalar.copy, turned_tile(G, "h_t2"))
-        acc1 = second_product((1, 3), 7)
+        weigh_on_vector(4, late([P, H], BF16, "h4", 33))
+        weigh_on_vector(5, late([P, H], BF16, "h5", 34))
+        quantise((1, 3), h_t1, late([P, G * P], U32, "h_w1", 24))
+        weigh_on_vector(7, late([P, H], BF16, "h7", 12))
+        h_t3 = {0: turn((6,), 3, nc.scalar.copy, turned_tile(1, "h_t30"))}
         store(0, acc0, nc.scalar.copy)
+        h_t2 = turn((4, 5), 0, nc.scalar.copy, turned_tile(G, "h_t2"))
+        h_t3[1] = turn((7,), 5, nc.scalar.copy, turned_tile(1, "h_t31"))
+        acc1 = second_product((1, 3), 7)
+        quantise((6,), h_t3[0], codes_tile(1, "h_w30"))
         quantise((4, 5), h_t2, codes_tile(G, "h_w2"))
-        store(1, acc1, nc.vector.tensor_copy)
+        quantise((7,), h_t3[1], codes_tile(1, "h_w31"))
+        store(1, acc1, nc.scalar.copy)
         acc2 = second_product((4, 5), 2)
         accs = [bank(b) for b in (1, 4, 6, 0)]
         for r in range(G):
-            group = (6 + r,)
-            quantise(group, turn(group, (3, 5)[r], nc.scalar.copy, turned_tile(1, f"h_t3{r}")), codes_tile(1, f"h_w3{r}"))
             for j in range(N // P):
-                second_pass(accs[j][:, 0:P], j, r, group, 0, P)
-        store(2, acc2, nc.scalar.copy)
+                second_pass(accs[j][:, 0:P], j, r, (6 + r,), 0, P)
+        store(2, acc2, nc.vector.tensor_copy)
         halves = [keep.tile([P, 2 * P], F32, name=f"half{i}") for i in range(2)]
         for j in range(N // P):
             dst = halves[j // 2][:, (j % 2) * P : (j % 2 + 1) * P]
-            if j == 2:
+            if j < 3:
                 nc.scalar.copy(dst, accs[j][:, 0:P])
             else:
                 nc.vector.tensor_copy(dst, accs[j][:, 0:P])

@@ -22,8 +22,7 @@ P = 128
 PASSES = K // 512
 TILES = T // P
 COLS = E * H
-X_ROW = 8
-W2_ROW = 12
+SPLIT = 5 * COLS // 8
 
 
 def tile_moe_wsel_b_relu2_p_kernel(
@@ -41,87 +40,105 @@ def tile_moe_wsel_b_relu2_p_kernel(
         def bank(b):
             return psum.tile([P, 512], F32, name=f"bank{b}", tag=f"bank{b}")
 
+        def shared(shape, dtype, name, kib):
+            return reuse.tile(shape, dtype, name=name, align_bytes=64, offset=1024 * kib)
+
         list1 = keep.tile([P, G * H // 16], U16, name="list1")
         list2 = keep.tile([P, G * N // 16], U16, name="list2")
         w1_all = [keep.tile([P, COLS], I32, name=f"w1_all{s}", align_bytes=64) for s in range(PASSES)]
-        w2_all = keep.tile([P, COLS], I32, name="w2_all", align_bytes=64)
-        x_w = [keep.tile([P, T], I32, name=f"x_w{s}", align_bytes=64) for s in range(PASSES)]
+        w2_all = shared([P, COLS], I32, "w2_all", 0)
+        x_w = {
+            (0, 0): keep.tile([P, T // 2], I32, name="x_w00", align_bytes=64),
+            (0, 1): keep.tile([P, T // 2], I32, name="x_w01", align_bytes=64),
+        }
+        x_w1 = keep.tile([P, T], I32, name="x_w1", align_bytes=64)
         w1s_all = keep.tile([P, COLS], U8, name="w1s_all", align_bytes=64)
         w2s_all = keep.tile([P, COLS], U8, name="w2s_all", align_bytes=64)
-        w1_s = keep.tile([P, G * H], U8, name="w1_s", align_bytes=64)
-        w2s_picked = reuse.tile([P, 3 * 1024], U8, name="w2s_picked", align_bytes=64, offset=32 * 1024)
+        w1s_picked = keep.tile([P, G * H], U8, name="w1s_picked", align_bytes=64)
+        w2s_picked = shared([P, G * N], U8, "w2s_picked", 12)
+        w1_s = keep.tile([P, PASSES * G * H], U8, name="w1_s", align_bytes=64)
         w2_s = keep.tile([P, G * N], U8, name="w2_s", align_bytes=64)
         x_s = keep.tile([P, PASSES * T], U8, name="x_s", align_bytes=64)
         gate_rows = keep.tile([P, P], F32, name="gate_rows")
         gate_cols = keep.tile([P, G * TILES], F32, name="gate_cols")
         ident = keep.tile([P, P], F32, name="ident")
 
-        nc.gpsimd.memset(w2s_all[:].bitcast(I32), 0)
-        nc.vector.memset(w1s_all[:].bitcast(I32), 0)
         nc.vector.memset(x_s[:].bitcast(I32), 0)
+        nc.vector.memset(w1s_all[0:96, :].bitcast(I32), 0)
+        nc.vector.memset(w1_s[:].bitcast(I32), 0)
         nc.gpsimd.memset(gate_rows[:], 0.0)
+        nc.gpsimd.memset(w2s_all[0:112, :].bitcast(I32), 0)
         nc.gpsimd.memset(w2_s[:].bitcast(I32), 0)
         make_identity(nc, ident[:])
 
-        nc.sync.dma_start(list2[:], offs2)
         nc.sync.dma_start(list1[:], offs)
-        nc.sync.dma_start(x_w[0][:], words(x_words[0]))
-        nc.sync.dma_start(w2s_all[0:P:8, :].bitcast(I32), w2_scales[0].bitcast(I32))
-        nc.sync.dma_start(
-            gate_rows[0 : G * TILES, :], gate[:, 0, :].rearrange("r (a c) -> r a c", c=P)
+        nc.scalar.dma_start(
+            w1s_all[96:P, :].bitcast(I32), w1_scales.rearrange("s b n -> b s n").bitcast(I32)
         )
-        for q in range(4):
-            nc.sync.dma_start(
-                w1s_all[32 * q : 32 * q + 4 * PASSES, :].bitcast(I32),
-                w1_scales[:, 4 * q : 4 * q + 4, :].bitcast(I32),
-            )
+        nc.sync.dma_start(list2[:], offs2)
+        nc.sync.dma_start(w1_all[0][:], words(w1_words[0]))
+        nc.scalar.dma_start(w2s_all[112:P, :].bitcast(I32), w2_scales[0].bitcast(I32))
         for j in range(4):
-            nc.sync.dma_start(
-                x_s[X_ROW + j : P : 32, :].bitcast(I32).rearrange("q (s t) -> q s t", s=PASSES),
+            nc.scalar.dma_start(
+                x_s[j:P:32, :].bitcast(I32).rearrange("q (s t) -> q s t", s=PASSES),
                 x_scales[:, j:16:4, :].rearrange("s q t -> q s t").bitcast(I32),
             )
-        for s in range(PASSES):
-            nc.sync.dma_start(w1_all[s][:], words(w1_words[s]))
-        nc.sync.dma_start(x_w[1][:], words(x_words[1]))
-        nc.sync.dma_start(w2_all[:], words(w2_words[0]))
+        nc.scalar.dma_start(
+            gate_rows[0 : G * TILES, :], gate[:, 0, :].rearrange("r (a c) -> r a c", c=P)
+        )
+        nc.sync.dma_start(x_w[0, 0][:], words(x_words[0])[:, 0 : T // 2])
+        nc.sync.dma_start(w1_all[1][:, 0 : SPLIT], words(w1_words[1])[:, 0 : SPLIT])
 
-        nc.vector.tensor_copy(w2s_picked[:, 0 : G * N], w2s_all[:].indirect(list2[:]))
+        nc.vector.tensor_copy(w1s_picked[:], w1s_all[:].indirect(list1[:]))
+        for q in range(4):
+            nc.sync.dma_start(
+                w1_s[32 * q : 32 * q + 4, :].bitcast(I32).rearrange("j (s n) -> j s n", s=PASSES),
+                w1s_picked[96 + 8 * q : 104 + 8 * q, :].bitcast(I32),
+            )
+        nc.sync.dma_start(w1_all[1][:, SPLIT : COLS], words(w1_words[1])[:, SPLIT : COLS])
+        nc.sync.dma_start(x_w1[:], words(x_words[1]))
+        nc.sync.dma_start(x_w[0, 1][:], words(x_words[0])[:, T // 2 : T])
+        nc.sync.dma_start(w2_all[:], words(w2_words[0]))
+        nc.vector.tensor_copy(w2s_picked[:], w2s_all[:].indirect(list2[:]))
         for j in range(4):
             nc.sync.dma_start(
-                w2_s[W2_ROW + j : P : 32, :].bitcast(I32),
-                w2s_picked[8 * j : P : 32, 0 : G * N].bitcast(I32),
+                w2_s[j:P:32, :].bitcast(I32), w2s_picked[112 + j : P : 4, :].bitcast(I32)
             )
 
         gate_t = bank(7)
         nc.tensor.transpose(gate_t[:, 0:P], gate_rows[:], ident[:])
         nc.scalar.copy(gate_cols[:], gate_t[:, 0 : G * TILES])
 
-        def gather_words(src, lst, r, name):
-            dst = keep.tile([P, 512], U32, name=name, align_bytes=64)
+        def gather_words(src, lst, r, dst):
             nc.vector.tensor_copy(dst[:], src[:].bitcast(U32).indirect(lst[:, r * 32 : (r + 1) * 32]))
             return dst
 
-        nc.vector.tensor_copy(w1_s[:], w1s_all[:].indirect(list1[:]))
         w1_w = {}
         for s in range(PASSES):
             for r in range(G):
-                w1_w[s, r] = gather_words(w1_all[s], list1, r, f"w1_w{s}{r}")
+                w1_w[s, r] = gather_words(
+                    w1_all[s], list1, r, keep.tile([P, H], U32, name=f"w1_w{s}{r}", align_bytes=64)
+                )
 
         units = [(0, 0), (1, 0), (0, 1), (1, 1), (2, 0), (2, 1), (3, 0), (3, 1)]
         pre = {}
         pos = {}
-        sq = {}
         hidden = {}
+        turned = {}
         codes = {}
 
         def first_pass(i, s):
             tt, r = units[i]
+            if s == 0:
+                tokens = x_w[0, tt // 2][:, (tt % 2) * P : (tt % 2 + 1) * P]
+            else:
+                tokens = x_w1[:, tt * P : (tt + 1) * P]
             nc.tensor.matmul_mx(
                 out=pre[i][:],
-                lhsT=x_w[s][:, tt * P : (tt + 1) * P].bitcast(FP8X4),
-                lhsT_scale=x_s[X_ROW:P, s * T + tt * P : s * T + (tt + 1) * P],
+                lhsT=tokens.bitcast(FP8X4),
+                lhsT_scale=x_s[:, s * T + tt * P : s * T + (tt + 1) * P],
                 rhs=w1_w[s, r][:].bitcast(FP8X4),
-                rhs_scale=w1_s[4 * s : P, r * H : (r + 1) * H],
+                rhs_scale=w1_s[:, s * G * H + r * H : s * G * H + (r + 1) * H],
                 start=(s == 0),
                 stop=(s == PASSES - 1),
             )
@@ -132,7 +149,7 @@ def tile_moe_wsel_b_relu2_p_kernel(
                 first_pass(i, s)
 
         def rectify(i):
-            pos[i] = late([P, H], F32, f"pos{i}", 16 + 2 * i)
+            pos[i] = keep.tile([P, H], F32, name=f"pos{i}")
             nc.scalar.activation(
                 pos[i][:].rearrange("t (u q e) -> t u q e", u=2, e=2),
                 pre[i][:].rearrange("t (q u e) -> t u q e", u=2, e=2),
@@ -143,99 +160,62 @@ def tile_moe_wsel_b_relu2_p_kernel(
             tt, r = units[i]
             return gate_cols[:, r * TILES + tt : r * TILES + tt + 1]
 
+        def h_tile(i):
+            return keep.tile([P, H], BF16, name=f"h{i}", align_bytes=64)
+
         def weigh_on_vector(i, h):
             hidden[i] = h
             nc.vector.scalar_tensor_tensor(h[:], pos[i][:], gate_col(i), pos[i][:], MULT, MULT)
 
-        def square(i):
-            sq[i] = keep.tile([P, H], F32, name=f"sq{i}")
-            nc.scalar.activation(sq[i][:], pos[i][:], SQUARE)
+        def weigh_on_scalar(i):
+            sq = keep.tile([P, H], F32, name=f"sq{i}")
+            hidden[i] = h_tile(i)
+            nc.scalar.activation(sq[:], pos[i][:], SQUARE)
+            nc.scalar.activation(hidden[i][:], sq[:], COPY, scale=gate_col(i))
 
-        def scale_on_scalar(i, h):
-            hidden[i] = h
-            nc.scalar.activation(h[:], sq[i][:], COPY, scale=gate_col(i))
-
-        def late(shape, dtype, name, slot):
-            return reuse.tile(shape, dtype, name=name, align_bytes=64, offset=1024 * slot)
-
-        def turned_tile(n, name):
-            return keep.tile([P, n * H], BF16, name=name, align_bytes=64)
-
-        def h_tile(i):
-            return keep.tile([P, H], BF16, name=f"h{i}", align_bytes=64)
-
-        def turn(group, b, copy, h_t):
+        def turn(group, b):
             n = len(group)
-            turned = bank(b)
+            into = bank(b)
             for m, i in enumerate(group):
                 for u in range(2):
                     nc.tensor.transpose(
-                        turned[:, (2 * m + u) * P : (2 * m + u + 1) * P],
+                        into[:, (2 * m + u) * P : (2 * m + u + 1) * P],
                         hidden[i][:].bitcast(F32)[:, u * P : (u + 1) * P],
                         ident[:],
                     )
-            copy(
-                h_t[:].bitcast(F32).rearrange("q (m t u) -> q m t u", m=n, u=2),
-                turned[:, 0 : 2 * n * P].rearrange("q (m u t) -> q m t u", m=n, u=2),
+            turned[group] = keep.tile([P, n * H], BF16, name=f"h_t{group[0]}", align_bytes=64)
+            nc.scalar.copy(
+                turned[group][:].bitcast(F32).rearrange("q (m t u) -> q m t u", m=n, u=2),
+                into[:, 0 : 2 * n * P].rearrange("q (m u t) -> q m t u", m=n, u=2),
             )
-            return h_t
 
-        def quantise(group, h_t, h_w):
-            n = len(group)
-            h_s = keep.tile([P, n * P], U8, name=f"h_s{group[0]}", align_bytes=64)
-            nc.vector.quantize_mx(out=h_w[:].bitcast(FP8X4), scales=h_s[:], in_=h_t[:])
+        def quantise(group, h_w):
+            h_s = keep.tile([P, len(group) * P], U8, name=f"h_s{group[0]}", align_bytes=64)
+            nc.vector.quantize_mx(out=h_w[:].bitcast(FP8X4), scales=h_s[:], in_=turned[group][:])
             codes[group] = (h_w, h_s)
+
+        def codes_tile(n, name):
+            return keep.tile([P, n * P], U32, name=name, align_bytes=64)
 
         out_view = out.rearrange("(j p) t -> p j t", p=P)
 
-        def second_pass(acc, j, r, group, lo, hi):
+        def second_pass(acc, j, r, group, m, start, stop):
             h_w, h_s = codes[group]
             nc.tensor.matmul_mx(
                 out=acc,
                 lhsT=w2_w[r][:, j * P : (j + 1) * P].bitcast(FP8X4),
-                lhsT_scale=w2_s[W2_ROW:P, r * N + j * P : r * N + (j + 1) * P],
-                rhs=h_w[:, lo:hi].bitcast(FP8X4),
-                rhs_scale=h_s[:, lo:hi],
-                start=(r == 0),
-                stop=(r == G - 1),
+                lhsT_scale=w2_s[:, r * N + j * P : r * N + (j + 1) * P],
+                rhs=h_w[:, m * P : (m + 1) * P].bitcast(FP8X4),
+                rhs_scale=h_s[:, m * P : (m + 1) * P],
+                start=start,
+                stop=stop,
             )
-
-        for i in range(4):
-            pre[i] = bank(i)
-        for s in range(PASSES):
-            for i in range(4):
-                first_pass(i, s)
-
-        rectify(0)
-        rectify(1)
-        first_product(4, 1)
-        weigh_on_vector(0, h_tile(0))
-        rectify(2)
-        first_product(5, 2)
-        weigh_on_vector(1, h_tile(1))
-        rectify(3)
-        weigh_on_vector(2, h_tile(2))
-        rectify(4)
-        first_product(6, 1)
-        weigh_on_vector(3, h_tile(3))
-        rectify(5)
-        h_t0 = turn((0, 2), 4, nc.scalar.copy, late([P, G * H], BF16, "h_t0", 12))
-        rectify(6)
-        first_product(7, 1)
-        h_t1 = turn((1, 3), 5, nc.scalar.copy, late([P, G * H], BF16, "h_t1", 14))
-        square(6)
-        rectify(7)
-        scale_on_scalar(6, h_tile(6))
-        w2_w = [gather_words(w2_all, list2, r, f"w2_w{r}") for r in range(G)]
-
-        def codes_tile(n, name):
-            return keep.tile([P, n * P], U32, name=name, align_bytes=64)
 
         def second_product(group, b):
             acc = bank(b)
             for j in range(N // P):
                 for r in range(G):
-                    second_pass(acc[:, j * P : (j + 1) * P], j, r, group, r * P, (r + 1) * P)
+                    second_pass(acc[:, j * P : (j + 1) * P], j, r, group, r, r == 0, r == G - 1)
             return acc
 
         def store(tt, acc, copy):
@@ -245,36 +225,58 @@ def tile_moe_wsel_b_relu2_p_kernel(
                 out_view[:, :, tt * P : (tt + 1) * P], res[:].rearrange("p (j t) -> p j t", t=P)
             )
 
-        quantise((0, 2), h_t0, late([P, G * P], U32, "h_w0", 32))
+        for i in range(4):
+            pre[i] = bank(i)
+        for s in range(PASSES):
+            for i in range(4):
+                first_pass(i, s)
+
+        rectify(0)
+        first_product(4, 0)
+        rectify(1)
+        first_product(5, 1)
+        weigh_on_vector(0, h_tile(0))
+        rectify(2)
+        weigh_on_vector(1, h_tile(1))
+        rectify(3)
+        weigh_on_vector(2, h_tile(2))
+        rectify(4)
+        first_product(6, 0)
+        rectify(5)
+        w2_w = [gather_words(w2_all, list2, r, shared([P, N], U32, f"w2_w{r}", 12 + 2 * r)) for r in range(G)]
+        turn((0, 2), 4)
+        first_product(7, 4)
+        weigh_on_scalar(3)
+        quantise((0, 2), shared([P, G * P], U32, "h_w0", 0))
         acc0 = second_product((0, 2), 6)
-        weigh_on_vector(4, late([P, H], BF16, "h4", 33))
-        weigh_on_vector(5, late([P, H], BF16, "h5", 34))
-        quantise((1, 3), h_t1, late([P, G * P], U32, "h_w1", 24))
-        weigh_on_vector(7, late([P, H], BF16, "h7", 12))
-        h_t3 = {0: turn((6,), 3, nc.scalar.copy, turned_tile(1, "h_t30"))}
-        store(0, acc0, nc.scalar.copy)
-        h_t2 = turn((4, 5), 0, nc.scalar.copy, turned_tile(G, "h_t2"))
-        h_t3[1] = turn((7,), 5, nc.scalar.copy, turned_tile(1, "h_t31"))
+        rectify(6)
+        turn((1, 3), 5)
+        rectify(7)
+        for i in range(4, 7):
+            weigh_on_vector(i, shared([P, H], BF16, f"h{i}", i))
+        quantise((1, 3), shared([P, G * P], U32, "h_w1", 1))
+        weigh_on_vector(7, shared([P, H], BF16, "h7", 7))
+        turn((4, 5), 2)
         acc1 = second_product((1, 3), 7)
-        quantise((6,), h_t3[0], codes_tile(1, "h_w30"))
-        quantise((4, 5), h_t2, codes_tile(G, "h_w2"))
-        quantise((7,), h_t3[1], codes_tile(1, "h_w31"))
+        turn((6,), 3)
+        store(0, acc0, nc.scalar.copy)
+        turn((7,), 1)
+        quantise((4, 5), codes_tile(G, "h_w2"))
+        acc2 = second_product((4, 5), 0)
+        quantise((6,), codes_tile(1, "h_w30"))
+        quantise((7,), codes_tile(1, "h_w31"))
         store(1, acc1, nc.scalar.copy)
-        acc2 = second_product((4, 5), 2)
-        accs = [bank(b) for b in (1, 4, 6, 0)]
+        accs = [bank(4), bank(5)]
         for r in range(G):
             for j in range(N // P):
-                second_pass(accs[j][:, 0:P], j, r, (6 + r,), 0, P)
+                c = j % 2
+                first, last = r == 0 and c == 0, r == G - 1 and c == 1
+                second_pass(accs[j // 2][:, c * P : (c + 1) * P], j, r, (6 + r,), 0, first, last)
         store(2, acc2, nc.vector.tensor_copy)
-        halves = [keep.tile([P, 2 * P], F32, name=f"half{i}") for i in range(2)]
-        for j in range(N // P):
-            dst = halves[j // 2][:, (j % 2) * P : (j % 2 + 1) * P]
-            if j < 3:
-                nc.scalar.copy(dst, accs[j][:, 0:P])
-            else:
-                nc.vector.tensor_copy(dst, accs[j][:, 0:P])
-            if j % 2 == 1:
-                nc.sync.dma_start(
-                    out_view[:, j - 1 : j + 1, 3 * P : 4 * P],
-                    halves[j // 2][:].rearrange("p (j t) -> p j t", t=P),
-                )
+        for half, copy in enumerate((nc.scalar.copy, nc.vector.tensor_copy)):
+            res = keep.tile([P, 2 * P], F32, name=f"half{half}")
+            copy(res[:], accs[half][:, 0 : 2 * P])
+            nc.sync.dma_start(
+                out_view[:, 2 * half : 2 * half + 2, 3 * P : 4 * P],
+                res[:].rearrange("p (j t) -> p j t", t=P),
+            )

@@ -15,8 +15,6 @@ U8 = mybir.dt.uint8
 FP8X4 = mybir.dt.float8_e4m3fn_x4
 MULT = mybir.AluOpType.mult
 RELU = mybir.ActivationFunctionType.Relu
-SQUARE = mybir.ActivationFunctionType.Square
-COPY = mybir.ActivationFunctionType.Copy
 
 P = 128
 PASSES = K // 512
@@ -167,12 +165,6 @@ def tile_moe_wsel_b_relu2_p_kernel(
             hidden[i] = h
             nc.vector.scalar_tensor_tensor(h[:], pos[i][:], gate_col(i), pos[i][:], MULT, MULT)
 
-        def weigh_on_scalar(i):
-            sq = keep.tile([P, H], F32, name=f"sq{i}")
-            hidden[i] = h_tile(i)
-            nc.scalar.activation(sq[:], pos[i][:], SQUARE)
-            nc.scalar.activation(hidden[i][:], sq[:], COPY, scale=gate_col(i))
-
         def turn(group, b):
             n = len(group)
             into = bank(b)
@@ -242,24 +234,25 @@ def tile_moe_wsel_b_relu2_p_kernel(
         weigh_on_vector(2, h_tile(2))
         rectify(4)
         first_product(6, 0)
+        weigh_on_vector(3, h_tile(3))
         rectify(5)
         w2_w = [gather_words(w2_all, list2, r, shared([P, N], U32, f"w2_w{r}", 12 + 2 * r)) for r in range(G)]
         turn((0, 2), 4)
         first_product(7, 4)
-        weigh_on_scalar(3)
-        quantise((0, 2), shared([P, G * P], U32, "h_w0", 0))
-        acc0 = second_product((0, 2), 6)
         rectify(6)
         turn((1, 3), 5)
         rectify(7)
-        for i in range(4, 7):
+        quantise((0, 2), shared([P, G * P], U32, "h_w0", 0))
+        acc0 = second_product((0, 2), 6)
+        for i in range(4, 6):
             weigh_on_vector(i, shared([P, H], BF16, f"h{i}", i))
         quantise((1, 3), shared([P, G * P], U32, "h_w1", 1))
-        weigh_on_vector(7, shared([P, H], BF16, "h7", 7))
+        for i in range(6, 8):
+            weigh_on_vector(i, shared([P, H], BF16, f"h{i}", i))
+        store(0, acc0, nc.scalar.copy)
         turn((4, 5), 2)
         acc1 = second_product((1, 3), 7)
         turn((6,), 3)
-        store(0, acc0, nc.scalar.copy)
         turn((7,), 1)
         quantise((4, 5), codes_tile(G, "h_w2"))
         acc2 = second_product((4, 5), 0)

@@ -20,7 +20,9 @@ P = 128
 PASSES = K // 512
 TILES = T // P
 COLS = E * H
-SPLIT = 5 * COLS // 8
+SPLIT = 3 * COLS // 8
+W1_ROW, W2_ROW = 4, 12
+WIDE = G * H + T
 
 
 def tile_moe_wsel_b_relu2_p_kernel(
@@ -44,7 +46,7 @@ def tile_moe_wsel_b_relu2_p_kernel(
         list1 = keep.tile([P, G * H // 16], U16, name="list1")
         list2 = keep.tile([P, G * N // 16], U16, name="list2")
         w1_all = [keep.tile([P, COLS], I32, name=f"w1_all{s}", align_bytes=64) for s in range(PASSES)]
-        w2_all = shared([P, COLS], I32, "w2_all", 0)
+        w2_all = keep.tile([P, COLS], I32, name="w2_all", align_bytes=64)
         x_w = {
             (0, 0): keep.tile([P, T // 2], I32, name="x_w00", align_bytes=64),
             (0, 1): keep.tile([P, T // 2], I32, name="x_w01", align_bytes=64),
@@ -52,21 +54,20 @@ def tile_moe_wsel_b_relu2_p_kernel(
         x_w1 = keep.tile([P, T], I32, name="x_w1", align_bytes=64)
         w1s_all = keep.tile([P, COLS], U8, name="w1s_all", align_bytes=64)
         w2s_all = keep.tile([P, COLS], U8, name="w2s_all", align_bytes=64)
-        w1s_picked = keep.tile([P, G * H], U8, name="w1s_picked", align_bytes=64)
-        w2s_picked = shared([P, G * N], U8, "w2s_picked", 12)
-        w1_s = keep.tile([P, PASSES * G * H], U8, name="w1_s", align_bytes=64)
+        w1s_picked = shared([P, G * H], U8, "w1s_picked", 0)
+        w2s_picked = shared([P, 5 * 1024], U8, "w2s_picked", 0)
+        staged = keep.tile([P, WIDE], U8, name="staged", align_bytes=64)
+        first_s = keep.tile([P, PASSES * WIDE], U8, name="first_s", align_bytes=64)
         w2_s = keep.tile([P, G * N], U8, name="w2_s", align_bytes=64)
-        x_s = keep.tile([P, PASSES * T], U8, name="x_s", align_bytes=64)
         gate_rows = keep.tile([P, P], F32, name="gate_rows")
         gate_cols = keep.tile([P, G * TILES], F32, name="gate_cols")
         ident = keep.tile([P, P], F32, name="ident")
 
-        nc.vector.memset(x_s[:].bitcast(I32), 0)
         nc.vector.memset(w1s_all[0:96, :].bitcast(I32), 0)
-        nc.vector.memset(w1_s[:].bitcast(I32), 0)
+        nc.vector.memset(first_s[:].bitcast(I32), 0)
+        nc.vector.memset(w2_s[:].bitcast(I32), 0)
         nc.gpsimd.memset(gate_rows[:], 0.0)
         nc.gpsimd.memset(w2s_all[0:112, :].bitcast(I32), 0)
-        nc.gpsimd.memset(w2_s[:].bitcast(I32), 0)
         make_identity(nc, ident[:])
 
         nc.sync.dma_start(list1[:], offs)
@@ -74,13 +75,11 @@ def tile_moe_wsel_b_relu2_p_kernel(
             w1s_all[96:P, :].bitcast(I32), w1_scales.rearrange("s b n -> b s n").bitcast(I32)
         )
         nc.sync.dma_start(list2[:], offs2)
+        nc.sync.dma_start(
+            staged[96:P, G * H : WIDE].bitcast(I32), x_scales.rearrange("s b t -> b s t").bitcast(I32)
+        )
         nc.sync.dma_start(w1_all[0][:], words(w1_words[0]))
         nc.scalar.dma_start(w2s_all[112:P, :].bitcast(I32), w2_scales[0].bitcast(I32))
-        for j in range(4):
-            nc.scalar.dma_start(
-                x_s[j:P:32, :].bitcast(I32).rearrange("q (s t) -> q s t", s=PASSES),
-                x_scales[:, j:16:4, :].rearrange("s q t -> q s t").bitcast(I32),
-            )
         nc.scalar.dma_start(
             gate_rows[0 : G * TILES, :], gate[:, 0, :].rearrange("r (a c) -> r a c", c=P)
         )
@@ -88,19 +87,22 @@ def tile_moe_wsel_b_relu2_p_kernel(
         nc.sync.dma_start(w1_all[1][:, 0 : SPLIT], words(w1_words[1])[:, 0 : SPLIT])
 
         nc.vector.tensor_copy(w1s_picked[:], w1s_all[:].indirect(list1[:]))
+        nc.vector.tensor_copy(staged[96:P, 0 : G * H].bitcast(I32), w1s_picked[96:P, :].bitcast(I32))
         for q in range(4):
             nc.sync.dma_start(
-                w1_s[32 * q : 32 * q + 4, :].bitcast(I32).rearrange("j (s n) -> j s n", s=PASSES),
-                w1s_picked[96 + 8 * q : 104 + 8 * q, :].bitcast(I32),
+                first_s[32 * q + W1_ROW : 32 * q + W1_ROW + 4, :]
+                .bitcast(I32)
+                .rearrange("j (s n) -> j s n", s=PASSES),
+                staged[96 + 8 * q : 104 + 8 * q, :].bitcast(I32),
             )
         nc.sync.dma_start(w1_all[1][:, SPLIT : COLS], words(w1_words[1])[:, SPLIT : COLS])
         nc.sync.dma_start(x_w1[:], words(x_words[1]))
         nc.sync.dma_start(x_w[0, 1][:], words(x_words[0])[:, T // 2 : T])
         nc.sync.dma_start(w2_all[:], words(w2_words[0]))
-        nc.vector.tensor_copy(w2s_picked[:], w2s_all[:].indirect(list2[:]))
+        nc.vector.tensor_copy(w2s_picked[:, 0 : G * N], w2s_all[:].indirect(list2[:]))
         for j in range(4):
             nc.sync.dma_start(
-                w2_s[j:P:32, :].bitcast(I32), w2s_picked[112 + j : P : 4, :].bitcast(I32)
+                w2_s[W2_ROW + j : P : 32, :].bitcast(I32), w2s_picked[112 + j : P : 4, 0 : G * N].bitcast(I32)
             )
 
         gate_t = bank(7)
@@ -134,9 +136,9 @@ def tile_moe_wsel_b_relu2_p_kernel(
             nc.tensor.matmul_mx(
                 out=pre[i][:],
                 lhsT=tokens.bitcast(FP8X4),
-                lhsT_scale=x_s[:, s * T + tt * P : s * T + (tt + 1) * P],
+                lhsT_scale=first_s[W1_ROW:P, s * WIDE + G * H + tt * P : s * WIDE + G * H + (tt + 1) * P],
                 rhs=w1_w[s, r][:].bitcast(FP8X4),
-                rhs_scale=w1_s[:, s * G * H + r * H : s * G * H + (r + 1) * H],
+                rhs_scale=first_s[W1_ROW:P, s * WIDE + r * H : s * WIDE + (r + 1) * H],
                 start=(s == 0),
                 stop=(s == PASSES - 1),
             )
@@ -196,7 +198,7 @@ def tile_moe_wsel_b_relu2_p_kernel(
             nc.tensor.matmul_mx(
                 out=acc,
                 lhsT=w2_w[r][:, j * P : (j + 1) * P].bitcast(FP8X4),
-                lhsT_scale=w2_s[:, r * N + j * P : r * N + (j + 1) * P],
+                lhsT_scale=w2_s[W2_ROW:P, r * N + j * P : r * N + (j + 1) * P],
                 rhs=h_w[:, m * P : (m + 1) * P].bitcast(FP8X4),
                 rhs_scale=h_s[:, m * P : (m + 1) * P],
                 start=start,
@@ -236,19 +238,22 @@ def tile_moe_wsel_b_relu2_p_kernel(
         first_product(6, 0)
         weigh_on_vector(3, h_tile(3))
         rectify(5)
-        w2_w = [gather_words(w2_all, list2, r, shared([P, N], U32, f"w2_w{r}", 12 + 2 * r)) for r in range(G)]
+        weigh_on_vector(4, h_tile(4))
+        w2_w = [
+            gather_words(w2_all, list2, r, keep.tile([P, N], U32, name=f"w2_w{r}", align_bytes=64))
+            for r in range(G)
+        ]
         turn((0, 2), 4)
         first_product(7, 4)
         rectify(6)
-        turn((1, 3), 5)
         rectify(7)
+        turn((1, 3), 5)
         quantise((0, 2), shared([P, G * P], U32, "h_w0", 0))
         acc0 = second_product((0, 2), 6)
-        for i in range(4, 6):
-            weigh_on_vector(i, shared([P, H], BF16, f"h{i}", i))
-        quantise((1, 3), shared([P, G * P], U32, "h_w1", 1))
-        for i in range(6, 8):
-            weigh_on_vector(i, shared([P, H], BF16, f"h{i}", i))
+        weigh_on_vector(5, shared([P, H], BF16, "h5", 1))
+        quantise((1, 3), shared([P, G * P], U32, "h_w1", 2))
+        weigh_on_vector(6, shared([P, H], BF16, "h6", 3))
+        weigh_on_vector(7, shared([P, H], BF16, "h7", 4))
         store(0, acc0, nc.scalar.copy)
         turn((4, 5), 2)
         acc1 = second_product((1, 3), 7)
@@ -257,15 +262,15 @@ def tile_moe_wsel_b_relu2_p_kernel(
         quantise((4, 5), codes_tile(G, "h_w2"))
         acc2 = second_product((4, 5), 0)
         quantise((6,), codes_tile(1, "h_w30"))
+        store(1, acc1, nc.vector.tensor_copy)
         quantise((7,), codes_tile(1, "h_w31"))
-        store(1, acc1, nc.scalar.copy)
         accs = [bank(4), bank(5)]
         for r in range(G):
             for j in range(N // P):
                 c = j % 2
                 first, last = r == 0 and c == 0, r == G - 1 and c == 1
                 second_pass(accs[j // 2][:, c * P : (c + 1) * P], j, r, (6 + r,), 0, first, last)
-        store(2, acc2, nc.vector.tensor_copy)
+        store(2, acc2, nc.scalar.copy)
         for half, copy in enumerate((nc.scalar.copy, nc.vector.tensor_copy)):
             res = keep.tile([P, 2 * P], F32, name=f"half{half}")
             copy(res[:], accs[half][:, 0 : 2 * P])

@@ -20,9 +20,9 @@ P = 128
 PASSES = K // 512
 TILES = T // P
 COLS = E * H
-SPLIT = 3 * COLS // 8
-W1_ROW, W2_ROW = 4, 12
-WIDE = G * H + T
+SPLIT = 7 * COLS // 16
+EARLY = 2 * P
+W1_ROW, X_ROW, W2_ROW = 4, 8, 12
 
 
 def tile_moe_wsel_b_relu2_p_kernel(
@@ -40,31 +40,32 @@ def tile_moe_wsel_b_relu2_p_kernel(
         def bank(b):
             return psum.tile([P, 512], F32, name=f"bank{b}", tag=f"bank{b}")
 
+        def own(shape, dtype, name):
+            return keep.tile(shape, dtype, name=name, align_bytes=64)
+
         def shared(shape, dtype, name, kib):
             return reuse.tile(shape, dtype, name=name, align_bytes=64, offset=1024 * kib)
 
         list1 = keep.tile([P, G * H // 16], U16, name="list1")
         list2 = keep.tile([P, G * N // 16], U16, name="list2")
-        w1_all = [keep.tile([P, COLS], I32, name=f"w1_all{s}", align_bytes=64) for s in range(PASSES)]
-        w2_all = keep.tile([P, COLS], I32, name="w2_all", align_bytes=64)
-        x_w = {
-            (0, 0): keep.tile([P, T // 2], I32, name="x_w00", align_bytes=64),
-            (0, 1): keep.tile([P, T // 2], I32, name="x_w01", align_bytes=64),
-        }
-        x_w1 = keep.tile([P, T], I32, name="x_w1", align_bytes=64)
-        w1s_all = keep.tile([P, COLS], U8, name="w1s_all", align_bytes=64)
-        w2s_all = keep.tile([P, COLS], U8, name="w2s_all", align_bytes=64)
-        w1s_picked = shared([P, G * H], U8, "w1s_picked", 0)
+        w1_all = [own([P, COLS], I32, "w1_all0"), own([P, COLS], I32, "w1_all1")]
+        w2_all = own([P, COLS], I32, "w2_all")
+        x_early = [own([P, EARLY], I32, f"x_early{s}") for s in range(PASSES)]
+        x_late = own([P, PASSES * (T - EARLY)], I32, "x_late")
+        w1s_all = own([P, COLS], U8, "w1s_all")
+        w2s_all = own([P, COLS], U8, "w2s_all")
+        w1s_picked = own([P, G * H], U8, "w1s_picked")
         w2s_picked = shared([P, 5 * 1024], U8, "w2s_picked", 0)
-        staged = keep.tile([P, WIDE], U8, name="staged", align_bytes=64)
-        first_s = keep.tile([P, PASSES * WIDE], U8, name="first_s", align_bytes=64)
-        w2_s = keep.tile([P, G * N], U8, name="w2_s", align_bytes=64)
-        gate_rows = keep.tile([P, P], F32, name="gate_rows")
-        gate_cols = keep.tile([P, G * TILES], F32, name="gate_cols")
-        ident = keep.tile([P, P], F32, name="ident")
+        x_s = own([P, PASSES * T], U8, "x_s")
+        w1_s = own([P, PASSES * G * H], U8, "w1_s")
+        w2_s = own([P, G * N], U8, "w2_s")
+        gate_rows = own([P, P], F32, "gate_rows")
+        gate_cols = own([P, G * TILES], F32, "gate_cols")
+        ident = own([P, P], F32, "ident")
 
+        nc.vector.memset(x_s[:].bitcast(I32), 0)
         nc.vector.memset(w1s_all[0:96, :].bitcast(I32), 0)
-        nc.vector.memset(first_s[:].bitcast(I32), 0)
+        nc.vector.memset(w1_s[:].bitcast(I32), 0)
         nc.vector.memset(w2_s[:].bitcast(I32), 0)
         nc.gpsimd.memset(gate_rows[:], 0.0)
         nc.gpsimd.memset(w2s_all[0:112, :].bitcast(I32), 0)
@@ -75,29 +76,33 @@ def tile_moe_wsel_b_relu2_p_kernel(
             w1s_all[96:P, :].bitcast(I32), w1_scales.rearrange("s b n -> b s n").bitcast(I32)
         )
         nc.sync.dma_start(list2[:], offs2)
-        nc.sync.dma_start(
-            staged[96:P, G * H : WIDE].bitcast(I32), x_scales.rearrange("s b t -> b s t").bitcast(I32)
-        )
         nc.sync.dma_start(w1_all[0][:], words(w1_words[0]))
         nc.scalar.dma_start(w2s_all[112:P, :].bitcast(I32), w2_scales[0].bitcast(I32))
-        nc.scalar.dma_start(
+        for q in range(4):
+            nc.scalar.dma_start(
+                x_s[32 * q + X_ROW : 32 * q + X_ROW + 4, :].bitcast(I32).rearrange("j (s t) -> j s t", s=PASSES),
+                x_scales[:, 4 * q : 4 * q + 4, :].rearrange("s j t -> j s t").bitcast(I32),
+            )
+        nc.gpsimd.dma_start(
             gate_rows[0 : G * TILES, :], gate[:, 0, :].rearrange("r (a c) -> r a c", c=P)
         )
-        nc.sync.dma_start(x_w[0, 0][:], words(x_words[0])[:, 0 : T // 2])
-        nc.sync.dma_start(w1_all[1][:, 0 : SPLIT], words(w1_words[1])[:, 0 : SPLIT])
+        nc.sync.dma_start(x_early[0][:], words(x_words[0])[:, 0:EARLY])
+        nc.sync.dma_start(w1_all[1][:, 0:SPLIT], words(w1_words[1])[:, 0:SPLIT])
 
         nc.vector.tensor_copy(w1s_picked[:], w1s_all[:].indirect(list1[:]))
-        nc.vector.tensor_copy(staged[96:P, 0 : G * H].bitcast(I32), w1s_picked[96:P, :].bitcast(I32))
         for q in range(4):
             nc.sync.dma_start(
-                first_s[32 * q + W1_ROW : 32 * q + W1_ROW + 4, :]
+                w1_s[32 * q + W1_ROW : 32 * q + W1_ROW + 4, :]
                 .bitcast(I32)
                 .rearrange("j (s n) -> j s n", s=PASSES),
-                staged[96 + 8 * q : 104 + 8 * q, :].bitcast(I32),
+                w1s_picked[96 + 8 * q : 104 + 8 * q, :].bitcast(I32),
             )
-        nc.sync.dma_start(w1_all[1][:, SPLIT : COLS], words(w1_words[1])[:, SPLIT : COLS])
-        nc.sync.dma_start(x_w1[:], words(x_words[1]))
-        nc.sync.dma_start(x_w[0, 1][:], words(x_words[0])[:, T // 2 : T])
+        nc.sync.dma_start(w1_all[1][:, SPLIT:COLS], words(w1_words[1])[:, SPLIT:COLS])
+        nc.sync.dma_start(x_early[1][:], words(x_words[1])[:, 0:EARLY])
+        nc.sync.dma_start(
+            x_late[:].rearrange("p (s t) -> p s t", s=PASSES),
+            x_words.rearrange("s p t d -> p s (t d)").bitcast(I32)[:, :, EARLY:T],
+        )
         nc.sync.dma_start(w2_all[:], words(w2_words[0]))
         nc.vector.tensor_copy(w2s_picked[:, 0 : G * N], w2s_all[:].indirect(list2[:]))
         for j in range(4):
@@ -109,172 +114,200 @@ def tile_moe_wsel_b_relu2_p_kernel(
         nc.tensor.transpose(gate_t[:, 0:P], gate_rows[:], ident[:])
         nc.scalar.copy(gate_cols[:], gate_t[:, 0 : G * TILES])
 
-        def gather_words(src, lst, r, dst):
-            nc.vector.tensor_copy(dst[:], src[:].bitcast(U32).indirect(lst[:, r * 32 : (r + 1) * 32]))
+        def gather_words(src, lst, first, count, name):
+            dst = own([P, count], U32, name)
+            nc.vector.tensor_copy(
+                dst[:], src[:].bitcast(U32).indirect(lst[:, first // 16 : (first + count) // 16])
+            )
             return dst
 
-        w1_w = {}
-        for s in range(PASSES):
-            for r in range(G):
-                w1_w[s, r] = gather_words(
-                    w1_all[s], list1, r, keep.tile([P, H], U32, name=f"w1_w{s}{r}", align_bytes=64)
-                )
+        half = H // 2
+        w1_first = [gather_words(w1_all[0], list1, r * H, H, f"w1_first{r}") for r in range(G)]
+        w1_second0 = [gather_words(w1_all[1], list1, a * half, half, f"w1_second0{a}") for a in range(2)]
+        w1_second1 = gather_words(w1_all[1], list1, H, H, "w1_second1")
 
-        units = [(0, 0), (1, 0), (0, 1), (1, 1), (2, 0), (2, 1), (3, 0), (3, 1)]
+        def first_pass(acc, tt, r, s, lo, hi, start, stop):
+            if tt * P < EARLY:
+                tokens = x_early[s][:, tt * P : (tt + 1) * P]
+            else:
+                at = s * (T - EARLY) + tt * P - EARLY
+                tokens = x_late[:, at : at + P]
+            if s == 0:
+                weights = w1_first[r][:, lo:hi]
+            else:
+                weights = w1_second0[lo // half][:] if r == 0 else w1_second1[:, lo:hi]
+            nc.tensor.matmul_mx(
+                out=acc,
+                lhsT=tokens.bitcast(FP8X4),
+                lhsT_scale=x_s[X_ROW:P, s * T + tt * P : s * T + (tt + 1) * P],
+                rhs=weights.bitcast(FP8X4),
+                rhs_scale=w1_s[W1_ROW:P, (s * G + r) * H + lo : (s * G + r) * H + hi],
+                start=start,
+                stop=stop,
+            )
+
         pre = {}
         pos = {}
         hidden = {}
         turned = {}
         codes = {}
 
-        def first_pass(i, s):
-            tt, r = units[i]
-            if s == 0:
-                tokens = x_w[0, tt // 2][:, (tt % 2) * P : (tt % 2 + 1) * P]
+        def open_unit(u, b):
+            pre[u] = bank(b)
+            first_pass(pre[u][:], u[0], u[1], 0, 0, H, True, False)
+
+        def close_unit(u):
+            if u[1] == 0:
+                for a in range(2):
+                    first_pass(pre[u][:, a * half : (a + 1) * half], u[0], 0, 1, a * half, (a + 1) * half, False, a == 1)
             else:
-                tokens = x_w1[:, tt * P : (tt + 1) * P]
-            nc.tensor.matmul_mx(
-                out=pre[i][:],
-                lhsT=tokens.bitcast(FP8X4),
-                lhsT_scale=first_s[W1_ROW:P, s * WIDE + G * H + tt * P : s * WIDE + G * H + (tt + 1) * P],
-                rhs=w1_w[s, r][:].bitcast(FP8X4),
-                rhs_scale=first_s[W1_ROW:P, s * WIDE + r * H : s * WIDE + (r + 1) * H],
-                start=(s == 0),
-                stop=(s == PASSES - 1),
-            )
+                first_pass(pre[u][:], u[0], 1, 1, 0, H, False, True)
 
-        def first_product(i, b):
-            pre[i] = bank(b)
-            for s in range(PASSES):
-                first_pass(i, s)
+        def first_product(u, b):
+            open_unit(u, b)
+            close_unit(u)
 
-        def rectify(i):
-            pos[i] = keep.tile([P, H], F32, name=f"pos{i}")
+        def gate_col(u):
+            return gate_cols[:, u[1] * TILES + u[0] : u[1] * TILES + u[0] + 1]
+
+        def rectify_part(u, src, a, parts):
+            n = P // parts
             nc.scalar.activation(
-                pos[i][:].rearrange("t (u q e) -> t u q e", u=2, e=2),
-                pre[i][:].rearrange("t (q u e) -> t u q e", u=2, e=2),
+                pos[u][:].rearrange("t (u q e) -> t u q e", u=2, e=2)[:, :, a * n : (a + 1) * n, :],
+                src.rearrange("t (q u e) -> t u q e", u=2, e=2),
                 RELU,
             )
 
-        def gate_col(i):
-            tt, r = units[i]
-            return gate_cols[:, r * TILES + tt : r * TILES + tt + 1]
+        def rectify(u):
+            pos[u] = own([P, H], F32, f"pos{u[0]}{u[1]}")
+            rectify_part(u, pre[u][:], 0, 1)
 
-        def h_tile(i):
-            return keep.tile([P, H], BF16, name=f"h{i}", align_bytes=64)
+        def h_tile(u):
+            return own([P, H], BF16, f"h{u[0]}{u[1]}")
 
-        def weigh_on_vector(i, h):
-            hidden[i] = h
-            nc.vector.scalar_tensor_tensor(h[:], pos[i][:], gate_col(i), pos[i][:], MULT, MULT)
+        def weigh(u, h):
+            hidden[u] = h
+            nc.vector.scalar_tensor_tensor(h[:], pos[u][:], gate_col(u), pos[u][:], MULT, MULT)
 
-        def turn(group, b):
-            n = len(group)
+        def turn(units, b):
+            tt = units[0][0]
+            if tt not in turned:
+                turned[tt] = own([P, G * H], BF16, f"turned{tt}")
+            n = len(units)
             into = bank(b)
-            for m, i in enumerate(group):
-                for u in range(2):
+            for m, u in enumerate(units):
+                pairs = hidden[u][:].bitcast(F32)
+                for w in range(2):
                     nc.tensor.transpose(
-                        into[:, (2 * m + u) * P : (2 * m + u + 1) * P],
-                        hidden[i][:].bitcast(F32)[:, u * P : (u + 1) * P],
-                        ident[:],
+                        into[:, (2 * m + w) * P : (2 * m + w + 1) * P], pairs[:, w * P : (w + 1) * P], ident[:]
                     )
-            turned[group] = keep.tile([P, n * H], BF16, name=f"h_t{group[0]}", align_bytes=64)
+            lo = units[0][1] * H
             nc.scalar.copy(
-                turned[group][:].bitcast(F32).rearrange("q (m t u) -> q m t u", m=n, u=2),
-                into[:, 0 : 2 * n * P].rearrange("q (m u t) -> q m t u", m=n, u=2),
+                turned[tt][:, lo : lo + n * H].bitcast(F32).rearrange("q (m t w) -> q m t w", m=n, w=2),
+                into[:, 0 : 2 * n * P].rearrange("q (m w t) -> q m t w", m=n, w=2),
             )
 
-        def quantise(group, h_w):
-            h_s = keep.tile([P, len(group) * P], U8, name=f"h_s{group[0]}", align_bytes=64)
-            nc.vector.quantize_mx(out=h_w[:].bitcast(FP8X4), scales=h_s[:], in_=turned[group][:])
-            codes[group] = (h_w, h_s)
-
-        def codes_tile(n, name):
-            return keep.tile([P, n * P], U32, name=name, align_bytes=64)
+        def quantise(tt, r, n, h_w):
+            h_s = own([P, n * P], U8, f"h_s{tt}{r}")
+            nc.vector.quantize_mx(
+                out=h_w[:].bitcast(FP8X4), scales=h_s[:], in_=turned[tt][:, r * H : (r + n) * H]
+            )
+            for m in range(n):
+                codes[tt, r + m] = (h_w[:, m * P : (m + 1) * P], h_s[:, m * P : (m + 1) * P])
 
         out_view = out.rearrange("(j p) t -> p j t", p=P)
 
-        def second_pass(acc, j, r, group, m, start, stop):
-            h_w, h_s = codes[group]
+        def second_pass(acc, tt, j, r, start, stop):
+            h_w, h_s = codes[tt, r]
             nc.tensor.matmul_mx(
                 out=acc,
-                lhsT=w2_w[r][:, j * P : (j + 1) * P].bitcast(FP8X4),
+                lhsT=w2_w[:, r * N + j * P : r * N + (j + 1) * P].bitcast(FP8X4),
                 lhsT_scale=w2_s[W2_ROW:P, r * N + j * P : r * N + (j + 1) * P],
-                rhs=h_w[:, m * P : (m + 1) * P].bitcast(FP8X4),
-                rhs_scale=h_s[:, m * P : (m + 1) * P],
+                rhs=h_w.bitcast(FP8X4),
+                rhs_scale=h_s,
                 start=start,
                 stop=stop,
             )
 
-        def second_product(group, b):
+        def second_product(tt, b):
             acc = bank(b)
             for j in range(N // P):
                 for r in range(G):
-                    second_pass(acc[:, j * P : (j + 1) * P], j, r, group, r, r == 0, r == G - 1)
+                    second_pass(acc[:, j * P : (j + 1) * P], tt, j, r, r == 0, r == G - 1)
             return acc
 
-        def store(tt, acc, copy):
-            res = keep.tile([P, N], F32, name=f"res{tt}")
-            copy(res[:], acc[:])
+        def store(tt, sums, first, blocks, copy):
+            res = own([P, blocks * P], F32, f"res{tt}{first}")
+            copy(res[:], sums)
             nc.sync.dma_start(
-                out_view[:, :, tt * P : (tt + 1) * P], res[:].rearrange("p (j t) -> p j t", t=P)
+                out_view[:, first : first + blocks, tt * P : (tt + 1) * P],
+                res[:].rearrange("p (j t) -> p j t", t=P),
             )
 
-        for i in range(4):
-            pre[i] = bank(i)
-        for s in range(PASSES):
-            for i in range(4):
-                first_pass(i, s)
-
-        rectify(0)
-        first_product(4, 0)
-        rectify(1)
-        first_product(5, 1)
-        weigh_on_vector(0, h_tile(0))
-        rectify(2)
-        weigh_on_vector(1, h_tile(1))
-        rectify(3)
-        weigh_on_vector(2, h_tile(2))
-        rectify(4)
-        first_product(6, 0)
-        weigh_on_vector(3, h_tile(3))
-        rectify(5)
-        weigh_on_vector(4, h_tile(4))
-        w2_w = [
-            gather_words(w2_all, list2, r, keep.tile([P, N], U32, name=f"w2_w{r}", align_bytes=64))
-            for r in range(G)
-        ]
-        turn((0, 2), 4)
-        first_product(7, 4)
-        rectify(6)
-        rectify(7)
-        turn((1, 3), 5)
-        quantise((0, 2), shared([P, G * P], U32, "h_w0", 0))
-        acc0 = second_product((0, 2), 6)
-        weigh_on_vector(5, shared([P, H], BF16, "h5", 1))
-        quantise((1, 3), shared([P, G * P], U32, "h_w1", 2))
-        weigh_on_vector(6, shared([P, H], BF16, "h6", 3))
-        weigh_on_vector(7, shared([P, H], BF16, "h7", 4))
-        store(0, acc0, nc.scalar.copy)
-        turn((4, 5), 2)
-        acc1 = second_product((1, 3), 7)
-        turn((6,), 3)
-        turn((7,), 1)
-        quantise((4, 5), codes_tile(G, "h_w2"))
-        acc2 = second_product((4, 5), 0)
-        quantise((6,), codes_tile(1, "h_w30"))
-        store(1, acc1, nc.vector.tensor_copy)
-        quantise((7,), codes_tile(1, "h_w31"))
-        accs = [bank(4), bank(5)]
-        for r in range(G):
+        def half_passes(accs, tt, r):
             for j in range(N // P):
                 c = j % 2
                 first, last = r == 0 and c == 0, r == G - 1 and c == 1
-                second_pass(accs[j // 2][:, c * P : (c + 1) * P], j, r, (6 + r,), 0, first, last)
-        store(2, acc2, nc.scalar.copy)
-        for half, copy in enumerate((nc.scalar.copy, nc.vector.tensor_copy)):
-            res = keep.tile([P, 2 * P], F32, name=f"half{half}")
-            copy(res[:], accs[half][:, 0 : 2 * P])
-            nc.sync.dma_start(
-                out_view[:, 2 * half : 2 * half + 2, 3 * P : 4 * P],
-                res[:].rearrange("p (j t) -> p j t", t=P),
-            )
+                second_pass(accs[j // 2][:, c * P : (c + 1) * P], tt, j, r, first, last)
+
+        halves = [bank(0), bank(1)]
+        for a in range(2):
+            first_pass(halves[a][:, 0:half], 0, 0, 0, a * half, (a + 1) * half, True, False)
+        open_unit((1, 0), 2)
+        open_unit((0, 1), 5)
+        for a in range(2):
+            first_pass(halves[a][:, 0:half], 0, 0, 1, a * half, (a + 1) * half, False, True)
+        close_unit((1, 0))
+
+        pos[0, 0] = own([P, H], F32, "pos00")
+        for a in range(2):
+            rectify_part((0, 0), halves[a][:, 0:half], a, 2)
+        open_unit((1, 1), 0)
+        close_unit((0, 1))
+        close_unit((1, 1))
+        first_product((2, 0), 1)
+        weigh((0, 0), h_tile((0, 0)))
+        rectify((1, 0))
+        first_product((2, 1), 2)
+        weigh((1, 0), h_tile((1, 0)))
+        for u in ((0, 1), (1, 1), (2, 0)):
+            rectify(u)
+            weigh(u, h_tile(u))
+        w2_w = gather_words(w2_all, list2, 0, G * N, "w2_w")
+        rectify((2, 1))
+        first_product((3, 0), 1)
+        turn(((0, 0), (0, 1)), 6)
+        rectify((3, 0))
+        first_product((3, 1), 6)
+        turn(((1, 0), (1, 1)), 7)
+        rectify((3, 1))
+        turn(((2, 0),), 3)
+
+        quantise(0, 0, G, shared([P, G * P], U32, "h_w0", 0))
+        acc0 = second_product(0, 5)
+        weigh((2, 1), shared([P, H], BF16, "h21", 4))
+        quantise(1, 0, G, shared([P, G * P], U32, "h_w1", 1))
+        store(0, acc0[:], 0, 4, nc.scalar.copy)
+        turn(((2, 1),), 4)
+        acc1 = second_product(1, 0)
+        weigh((3, 0), shared([P, H], BF16, "h30", 2))
+        weigh((3, 1), shared([P, H], BF16, "h31", 3))
+        store(1, acc1[:, 0 : 2 * P], 0, 2, nc.scalar.copy)
+        turn(((3, 0),), 7)
+        turn(((3, 1),), 3)
+        quantise(2, 0, G, own([P, G * P], U32, "h_w2"))
+        acc2 = [bank(2), bank(5)]
+        for c in range(2):
+            for j in range(2):
+                for r in range(G):
+                    second_pass(acc2[c][:, j * P : (j + 1) * P], 2, 2 * c + j, r, r == 0, r == G - 1)
+        store(1, acc1[:, 2 * P : 4 * P], 2, 2, nc.vector.tensor_copy)
+        quantise(3, 0, 1, own([P, P], U32, "h_w30"))
+        quantise(3, 1, 1, own([P, P], U32, "h_w31"))
+        acc3 = [bank(1), bank(6)]
+        for r in range(G):
+            half_passes(acc3, 3, r)
+        for c in range(2):
+            store(2, acc2[c][:, 0 : 2 * P], 2 * c, 2, nc.scalar.copy)
+        store(3, acc3[0][:, 0 : 2 * P], 0, 2, nc.vector.tensor_copy)
+        store(3, acc3[1][:, 0 : 2 * P], 2, 2, nc.scalar.copy)

@@ -57,7 +57,7 @@ def tile_moe_wsel_b_relu2_p_kernel(
         w1s_picked = own([P, G * H], U8, "w1s_picked")
         w2s_picked = shared([P, 5 * 1024], U8, "w2s_picked", 0)
         x_s = own([P, PASSES * T], U8, "x_s")
-        w1_s = own([P, PASSES * G * H], U8, "w1_s")
+        w1_s = [own([P, G * H], U8, f"w1_s{s}") for s in range(PASSES)]
         w2_s = own([P, G * N], U8, "w2_s")
         gate_rows = own([P, P], F32, "gate_rows")
         gate_cols = own([P, G * TILES], F32, "gate_cols")
@@ -65,7 +65,8 @@ def tile_moe_wsel_b_relu2_p_kernel(
 
         nc.vector.memset(x_s[:].bitcast(I32), 0)
         nc.vector.memset(w1s_all[0:96, :].bitcast(I32), 0)
-        nc.vector.memset(w1_s[:].bitcast(I32), 0)
+        for s in range(PASSES):
+            nc.vector.memset(w1_s[s][:].bitcast(I32), 0)
         nc.vector.memset(w2_s[:].bitcast(I32), 0)
         nc.gpsimd.memset(gate_rows[:], 0.0)
         nc.gpsimd.memset(w2s_all[0:112, :].bitcast(I32), 0)
@@ -90,14 +91,17 @@ def tile_moe_wsel_b_relu2_p_kernel(
         nc.sync.dma_start(w1_all[1][:, 0:SPLIT], words(w1_words[1])[:, 0:SPLIT])
 
         nc.vector.tensor_copy(w1s_picked[:], w1s_all[:].indirect(list1[:]))
-        for q in range(4):
-            nc.sync.dma_start(
-                w1_s[32 * q + W1_ROW : 32 * q + W1_ROW + 4, :]
-                .bitcast(I32)
-                .rearrange("j (s n) -> j s n", s=PASSES),
-                w1s_picked[96 + 8 * q : 104 + 8 * q, :].bitcast(I32),
-            )
+
+        def move_scales(s):
+            for q in range(4):
+                nc.sync.dma_start(
+                    w1_s[s][32 * q + W1_ROW : 32 * q + W1_ROW + 4, :].bitcast(I32),
+                    w1s_picked[96 + 8 * q + s : 104 + 8 * q : 2, :].bitcast(I32),
+                )
+
+        move_scales(0)
         nc.sync.dma_start(w1_all[1][:, SPLIT:COLS], words(w1_words[1])[:, SPLIT:COLS])
+        move_scales(1)
         nc.sync.dma_start(x_early[1][:], words(x_words[1])[:, 0:EARLY])
         nc.sync.dma_start(
             x_late[:].rearrange("p (s t) -> p s t", s=PASSES),
@@ -141,7 +145,7 @@ def tile_moe_wsel_b_relu2_p_kernel(
                 lhsT=tokens.bitcast(FP8X4),
                 lhsT_scale=x_s[X_ROW:P, s * T + tt * P : s * T + (tt + 1) * P],
                 rhs=weights.bitcast(FP8X4),
-                rhs_scale=w1_s[W1_ROW:P, (s * G + r) * H + lo : (s * G + r) * H + hi],
+                rhs_scale=w1_s[s][W1_ROW:P, r * H + lo : r * H + hi],
                 start=start,
                 stop=stop,
             )

@@ -52,25 +52,22 @@ def tile_moe_wsel_b_relu2_p_kernel(
         w2_all = own([P, COLS], I32, "w2_all")
         x_early = [own([P, EARLY], I32, f"x_early{s}") for s in range(PASSES)]
         x_late = own([P, PASSES * (T - EARLY)], I32, "x_late")
-        w1s_all = own([P, COLS], U8, "w1s_all")
+        w1s_all = shared([P, COLS], U8, "w1s_all", 8)
         w2s_all = own([P, COLS], U8, "w2s_all")
         w1s_picked = own([P, G * H], U8, "w1s_picked")
         w2s_picked = shared([P, 5 * 1024], U8, "w2s_picked", 0)
         x_s = own([P, PASSES * T], U8, "x_s")
-        w1_s = [own([P, G * H], U8, f"w1_s{s}") for s in range(PASSES)]
-        w2_s = own([P, G * N], U8, "w2_s")
+        w1_s = [own([P, G * H], U8, "w1_s0"), shared([P, G * H], U8, "w1_s1", 8)]
+        w2_s = shared([P, G * N], U8, "w2_s", 9)
         gate_rows = own([P, P], F32, "gate_rows")
         gate_cols = own([P, G * TILES], F32, "gate_cols")
         ident = own([P, P], F32, "ident")
 
-        nc.vector.memset(x_s[:].bitcast(I32), 0)
         nc.vector.memset(w1s_all[0:96, :].bitcast(I32), 0)
-        for s in range(PASSES):
-            nc.vector.memset(w1_s[s][:].bitcast(I32), 0)
-        nc.vector.memset(w2_s[:].bitcast(I32), 0)
+        nc.vector.memset(x_s[:].bitcast(I32), 0)
+        nc.vector.memset(w1_s[0][:].bitcast(I32), 0)
+        nc.vector.memset(w2s_all[0:112, :].bitcast(I32), 0)
         nc.gpsimd.memset(gate_rows[:], 0.0)
-        nc.gpsimd.memset(w2s_all[0:112, :].bitcast(I32), 0)
-        make_identity(nc, ident[:])
 
         nc.sync.dma_start(list1[:], offs)
         nc.scalar.dma_start(
@@ -87,10 +84,13 @@ def tile_moe_wsel_b_relu2_p_kernel(
         nc.gpsimd.dma_start(
             gate_rows[0 : G * TILES, :], gate[:, 0, :].rearrange("r (a c) -> r a c", c=P)
         )
+        make_identity(nc, ident[:])
         nc.sync.dma_start(x_early[0][:], words(x_words[0])[:, 0:EARLY])
         nc.sync.dma_start(w1_all[1][:, 0:SPLIT], words(w1_words[1])[:, 0:SPLIT])
 
         nc.vector.tensor_copy(w1s_picked[:], w1s_all[:].indirect(list1[:]))
+        nc.vector.memset(w1_s[1][:].bitcast(I32), 0)
+        nc.vector.memset(w2_s[:].bitcast(I32), 0)
 
         def move_scales(s):
             for q in range(4):

@@ -89,8 +89,6 @@ def tile_moe_wsel_b_relu2_p_kernel(
         nc.sync.dma_start(w1_all[1][:, 0:SPLIT], words(w1_words[1])[:, 0:SPLIT])
 
         nc.vector.tensor_copy(w1s_picked[:], w1s_all[:].indirect(list1[:]))
-        nc.vector.memset(w1_s[1][:].bitcast(I32), 0)
-        nc.vector.memset(w2_s[:].bitcast(I32), 0)
 
         def move_scales(s):
             for q in range(4):

@@ -252,6 +252,18 @@ def tile_moe_wsel_b_relu2_p_kernel(
                 first, last = r == 0 and c == 0, r == G - 1 and c == 1
                 second_pass(accs[j // 2][:, c * P : (c + 1) * P], tt, j, r, first, last)
 
+        idle = bank(4)
+        for a in range(4):
+            nc.tensor.matmul_mx(
+                out=idle[:, (a % 2) * half : (a % 2 + 1) * half],
+                lhsT=x_early[0][:, 0:P].bitcast(FP8X4),
+                lhsT_scale=x_s[X_ROW:P, 0:P],
+                rhs=x_early[0][:].bitcast(FP8X4),
+                rhs_scale=x_s[X_ROW:P, 0:EARLY],
+                start=True,
+                stop=True,
+            )
+
         halves = [bank(0), bank(1)]
         for a in range(2):
             first_pass(halves[a][:, 0:half], 0, 0, 0, a * half, (a + 1) * half, True, False)

from contextlib import ExitStack

import concourse.mybir as mybir
from concourse.masks import make_identity

K, T, E, G, H, N = 1024, 512, 6, 2, 512, 512
FLOPS = 2 * G * T * (K * H + H * N)

F32 = mybir.dt.float32
BF16 = mybir.dt.bfloat16
I32 = mybir.dt.int32
U32 = mybir.dt.uint32
U16 = mybir.dt.uint16
U8 = mybir.dt.uint8
FP8X4 = mybir.dt.float8_e4m3fn_x4
MULT = mybir.AluOpType.mult
RELU = mybir.ActivationFunctionType.Relu

P = 128
PASSES = K // 512
TILES = T // P
COLS = E * H
SPLIT = 7 * COLS // 16
EARLY = 2 * P
W1_ROW, X_ROW, W2_ROW = 4, 8, 12


def tile_moe_wsel_b_relu2_p_kernel(
    tc, x_words, x_scales, w1_words, w1_scales, w2_words, w2_scales, gate, offs, offs2, out
):
    nc = tc.nc
    with ExitStack() as ctx:
        keep = ctx.enter_context(tc.tile_pool(name="keep", bufs=1))
        reuse = ctx.enter_context(tc.tile_pool(name="reuse", bufs=1))
        psum = ctx.enter_context(tc.psum_pool(name="psum", bufs=1))

        def words(dram):
            return dram.rearrange("p n d -> p (n d)").bitcast(I32)

        def bank(b):
            return psum.tile([P, 512], F32, name=f"bank{b}", tag=f"bank{b}")

        def own(shape, dtype, name):
            return keep.tile(shape, dtype, name=name, align_bytes=64)

        def shared(shape, dtype, name, kib):
            return reuse.tile(shape, dtype, name=name, align_bytes=64, offset=1024 * kib)

        list1 = keep.tile([P, G * H // 16], U16, name="list1")
        list2 = keep.tile([P, G * N // 16], U16, name="list2")
        w1_all = [own([P, COLS], I32, "w1_all0"), own([P, COLS], I32, "w1_all1")]
        w2_all = own([P, COLS], I32, "w2_all")
        x_early = [own([P, EARLY], I32, f"x_early{s}") for s in range(PASSES)]
        x_late = own([P, PASSES * (T - EARLY)], I32, "x_late")
        w1s_all = shared([P, COLS], U8, "w1s_all", 8)
        w2s_all = own([P, COLS], U8, "w2s_all")
        w1s_picked = own([P, G * H], U8, "w1s_picked")
        w2s_picked = shared([P, 5 * 1024], U8, "w2s_picked", 0)
        x_s = own([P, PASSES * T], U8, "x_s")
        w1_s = [own([P, G * H], U8, "w1_s0"), shared([P, G * H], U8, "w1_s1", 8)]
        w2_s = shared([P, G * N], U8, "w2_s", 9)
        gate_rows = own([P, P], F32, "gate_rows")
        gate_cols = own([P, G * TILES], F32, "gate_cols")
        ident = own([P, P], F32, "ident")

        nc.vector.memset(w1s_all[0:96, :].bitcast(I32), 0)
        nc.vector.memset(x_s[:].bitcast(I32), 0)
        nc.vector.memset(w1_s[0][:].bitcast(I32), 0)
        nc.vector.memset(w2s_all[0:112, :].bitcast(I32), 0)
        nc.gpsimd.memset(gate_rows[:], 0.0)

        nc.sync.dma_start(list1[:], offs)
        nc.scalar.dma_start(
            w1s_all[96:P, :].bitcast(I32), w1_scales.rearrange("s b n -> b s n").bitcast(I32)
        )
        nc.sync.dma_start(list2[:], offs2)
        nc.sync.dma_start(w1_all[0][:], words(w1_words[0]))
        nc.scalar.dma_start(w2s_all[112:P, :].bitcast(I32), w2_scales[0].bitcast(I32))
        for q in range(4):
            nc.scalar.dma_start(
                x_s[32 * q + X_ROW : 32 * q + X_ROW + 4, :].bitcast(I32).rearrange("j (s t) -> j s t", s=PASSES),
                x_scales[:, 4 * q : 4 * q + 4, :].rearrange("s j t -> j s t").bitcast(I32),
            )
        nc.gpsimd.dma_start(
            gate_rows[0 : G * TILES, :], gate[:, 0, :].rearrange("r (a c) -> r a c", c=P)
        )
        make_identity(nc, ident[:])
        nc.sync.dma_start(x_early[0][:], words(x_words[0])[:, 0:EARLY])
        nc.sync.dma_start(w1_all[1][:, 0:SPLIT], words(w1_words[1])[:, 0:SPLIT])

        nc.vector.tensor_copy(w1s_picked[:], w1s_all[:].indirect(list1[:]))

        def move_scales(s):
            for q in range(4):
                nc.sync.dma_start(
                    w1_s[s][32 * q + W1_ROW : 32 * q + W1_ROW + 4, :].bitcast(I32),
                    w1s_picked[96 + 8 * q + s : 104 + 8 * q : 2, :].bitcast(I32),
                )

        move_scales(0)
        nc.sync.dma_start(w1_all[1][:, SPLIT:COLS], words(w1_words[1])[:, SPLIT:COLS])
        move_scales(1)
        nc.sync.dma_start(x_early[1][:], words(x_words[1])[:, 0:EARLY])
        nc.sync.dma_start(
            x_late[:].rearrange("p (s t) -> p s t", s=PASSES),
            x_words.rearrange("s p t d -> p s (t d)").bitcast(I32)[:, :, EARLY:T],
        )
        nc.sync.dma_start(w2_all[:], words(w2_words[0]))
        nc.vector.tensor_copy(w2s_picked[:, 0 : G * N], w2s_all[:].indirect(list2[:]))
        for j in range(4):
            nc.sync.dma_start(
                w2_s[W2_ROW + j : P : 32, :].bitcast(I32), w2s_picked[112 + j : P : 4, 0 : G * N].bitcast(I32)
            )

        gate_t = bank(7)
        nc.tensor.transpose(gate_t[:, 0:P], gate_rows[:], ident[:])
        nc.scalar.copy(gate_cols[:], gate_t[:, 0 : G * TILES])

        def gather_words(src, lst, first, count, name):
            dst = own([P, count], U32, name)
            nc.vector.tensor_copy(
                dst[:], src[:].bitcast(U32).indirect(lst[:, first // 16 : (first + count) // 16])
            )
            return dst

        half = H // 2
        w1_first = [gather_words(w1_all[0], list1, r * H, H, f"w1_first{r}") for r in range(G)]
        w1_second0 = [gather_words(w1_all[1], list1, a * half, half, f"w1_second0{a}") for a in range(2)]
        w1_second1 = gather_words(w1_all[1], list1, H, H, "w1_second1")

        def first_pass(acc, tt, r, s, lo, hi, start, stop):
            if tt * P < EARLY:
                tokens = x_early[s][:, tt * P : (tt + 1) * P]
            else:
                at = s * (T - EARLY) + tt * P - EARLY
                tokens = x_late[:, at : at + P]
            if s == 0:
                weights = w1_first[r][:, lo:hi]
            else:
                weights = w1_second0[lo // half][:] if r == 0 else w1_second1[:, lo:hi]
            nc.tensor.matmul_mx(
                out=acc,
                lhsT=tokens.bitcast(FP8X4),
                lhsT_scale=x_s[X_ROW:P, s * T + tt * P : s * T + (tt + 1) * P],
                rhs=weights.bitcast(FP8X4),
                rhs_scale=w1_s[s][W1_ROW:P, r * H + lo : r * H + hi],
                start=start,
                stop=stop,
            )

        pre = {}
        pos = {}
        hidden = {}
        turned = {}
        codes = {}

        def open_unit(u, b):
            pre[u] = bank(b)
            first_pass(pre[u][:], u[0], u[1], 0, 0, H, True, False)

        def close_unit(u):
            if u[1] == 0:
                for a in range(2):
                    first_pass(pre[u][:, a * half : (a + 1) * half], u[0], 0, 1, a * half, (a + 1) * half, False, a == 1)
            else:
                first_pass(pre[u][:], u[0], 1, 1, 0, H, False, True)

        def first_product(u, b):
            open_unit(u, b)
            close_unit(u)

        def gate_col(u):
            return gate_cols[:, u[1] * TILES + u[0] : u[1] * TILES + u[0] + 1]

        def rectify_part(u, src, a, parts):
            n = P // parts
            nc.scalar.activation(
                pos[u][:].rearrange("t (u q e) -> t u q e", u=2, e=2)[:, :, a * n : (a + 1) * n, :],
                src.rearrange("t (q u e) -> t u q e", u=2, e=2),
                RELU,
            )

        def rectify(u):
            pos[u] = own([P, H], F32, f"pos{u[0]}{u[1]}")
            rectify_part(u, pre[u][:], 0, 1)

        def h_tile(u):
            return own([P, H], BF16, f"h{u[0]}{u[1]}")

        def weigh(u, h):
            hidden[u] = h
            nc.vector.scalar_tensor_tensor(h[:], pos[u][:], gate_col(u), pos[u][:], MULT, MULT)

        def turn(units, b):
            tt = units[0][0]
            if tt not in turned:
                turned[tt] = own([P, G * H], BF16, f"turned{tt}")
            n = len(units)
            into = bank(b)
            for m, u in enumerate(units):
                pairs = hidden[u][:].bitcast(F32)
                for w in range(2):
                    nc.tensor.transpose(
                        into[:, (2 * m + w) * P : (2 * m + w + 1) * P], pairs[:, w * P : (w + 1) * P], ident[:]
                    )
            lo = units[0][1] * H
            nc.scalar.copy(
                turned[tt][:, lo : lo + n * H].bitcast(F32).rearrange("q (m t w) -> q m t w", m=n, w=2),
                into[:, 0 : 2 * n * P].rearrange("q (m w t) -> q m t w", m=n, w=2),
            )

        def quantise(tt, r, n, h_w):
            h_s = own([P, n * P], U8, f"h_s{tt}{r}")
            nc.vector.quantize_mx(
                out=h_w[:].bitcast(FP8X4), scales=h_s[:], in_=turned[tt][:, r * H : (r + n) * H]
            )
            for m in range(n):
                codes[tt, r + m] = (h_w[:, m * P : (m + 1) * P], h_s[:, m * P : (m + 1) * P])

        out_view = out.rearrange("(j p) t -> p j t", p=P)

        def second_pass(acc, tt, j, r, start, stop):
            h_w, h_s = codes[tt, r]
            nc.tensor.matmul_mx(
                out=acc,
                lhsT=w2_w[:, r * N + j * P : r * N + (j + 1) * P].bitcast(FP8X4),
                lhsT_scale=w2_s[W2_ROW:P, r * N + j * P : r * N + (j + 1) * P],
                rhs=h_w.bitcast(FP8X4),
                rhs_scale=h_s,
                start=start,
                stop=stop,
            )

        def second_product(tt, b):
            acc = bank(b)
            for j in range(N // P):
                for r in range(G):
                    second_pass(acc[:, j * P : (j + 1) * P], tt, j, r, r == 0, r == G - 1)
            return acc

        def store(tt, sums, first, blocks, copy):
            res = own([P, blocks * P], F32, f"res{tt}{first}")
            copy(res[:], sums)
            nc.sync.dma_start(
                out_view[:, first : first + blocks, tt * P : (tt + 1) * P],
                res[:].rearrange("p (j t) -> p j t", t=P),
            )

        def half_passes(accs, tt, r):
            for j in range(N // P):
                c = j % 2
                first, last = r == 0 and c == 0, r == G - 1 and c == 1
                second_pass(accs[j // 2][:, c * P : (c + 1) * P], tt, j, r, first, last)

        idle = bank(4)
        for a in range(4):
            nc.tensor.matmul_mx(
                out=idle[:, (a % 2) * half : (a % 2 + 1) * half],
                lhsT=x_early[0][:, 0:P].bitcast(FP8X4),
                lhsT_scale=x_s[X_ROW:P, 0:P],
                rhs=x_early[0][:].bitcast(FP8X4),
                rhs_scale=x_s[X_ROW:P, 0:EARLY],
                start=True,
                stop=True,
            )

        halves = [bank(0), bank(1)]
        for a in range(2):
            first_pass(halves[a][:, 0:half], 0, 0, 0, a * half, (a + 1) * half, True, False)
        open_unit((1, 0), 2)
        open_unit((0, 1), 5)
        for a in range(2):
            first_pass(halves[a][:, 0:half], 0, 0, 1, a * half, (a + 1) * half, False, True)
        close_unit((1, 0))

        pos[0, 0] = own([P, H], F32, "pos00")
        for a in range(2):
            rectify_part((0, 0), halves[a][:, 0:half], a, 2)
        open_unit((1, 1), 0)
        close_unit((0, 1))
        close_unit((1, 1))
        first_product((2, 0), 1)
        weigh((0, 0), h_tile((0, 0)))
        rectify((1, 0))
        first_product((2, 1), 2)
        weigh((1, 0), h_tile((1, 0)))
        for u in ((0, 1), (1, 1), (2, 0)):
            rectify(u)
            weigh(u, h_tile(u))
        w2_w = gather_words(w2_all, list2, 0, G * N, "w2_w")
        rectify((2, 1))
        first_product((3, 0), 1)
        turn(((0, 0), (0, 1)), 6)
        rectify((3, 0))
        first_product((3, 1), 6)
        turn(((1, 0), (1, 1)), 7)
        rectify((3, 1))
        turn(((2, 0),), 3)

        quantise(0, 0, G, shared([P, G * P], U32, "h_w0", 0))
        acc0 = second_product(0, 5)
        weigh((2, 1), shared([P, H], BF16, "h21", 4))
        quantise(1, 0, G, shared([P, G * P], U32, "h_w1", 1))
        store(0, acc0[:], 0, 4, nc.scalar.copy)
        turn(((2, 1),), 4)
        acc1 = second_product(1, 0)
        weigh((3, 0), shared([P, H], BF16, "h30", 2))
        weigh((3, 1), shared([P, H], BF16, "h31", 3))
        store(1, acc1[:, 0 : 2 * P], 0, 2, nc.scalar.copy)
        turn(((3, 0),), 7)
        turn(((3, 1),), 3)
        quantise(2, 0, G, own([P, G * P], U32, "h_w2"))
        acc2 = [bank(2), bank(5)]
        for c in range(2):
            for j in range(2):
                for r in range(G):
                    second_pass(acc2[c][:, j * P : (j + 1) * P], 2, 2 * c + j, r, r == 0, r == G - 1)
        store(1, acc1[:, 2 * P : 4 * P], 2, 2, nc.vector.tensor_copy)
        quantise(3, 0, 1, own([P, P], U32, "h_w30"))
        quantise(3, 1, 1, own([P, P], U32, "h_w31"))
        acc3 = [bank(1), bank(6)]
        for r in range(G):
            half_passes(acc3, 3, r)
        for c in range(2):
            store(2, acc2[c][:, 0 : 2 * P], 2 * c, 2, nc.scalar.copy)
        store(3, acc3[0][:, 0 : 2 * P], 0, 2, nc.vector.tensor_copy)
        store(3, acc3[1][:, 0 : 2 * P], 2, 2, nc.scalar.copy)
